import numpy as np
import ml_dtypes


def mxq(x, axis, fmt="e4m3"):
    dtype, down = {"e4m3": (ml_dtypes.float8_e4m3fn, 7), "e5m2": (ml_dtypes.float8_e5m2, 14)}[fmt]
    v = np.moveaxis(np.asarray(x, np.float32).astype(ml_dtypes.bfloat16).astype(np.float64), axis, -1)
    blocks = v.reshape(v.shape[:-1] + (-1, 32))
    amax = np.abs(blocks).max(-1, keepdims=True)
    byte = np.maximum(np.where(amax > 0, np.frexp(amax)[1] - 1 + 127, 0) - down, 1)
    scale = np.exp2(byte - 127.0)
    codes = (blocks / scale).astype(np.float32).astype(dtype).astype(np.float64)
    return np.moveaxis((codes * scale).reshape(v.shape), -1, axis)


WIDE = False


def mx_kscale(k):
    if not WIDE:
        return np.ones(k)
    levels = np.array([10, -10, 5, -5, 0])
    if k % 512:
        return np.exp2(np.random.permutation(np.resize(levels, k // 32))).repeat(32)
    a = np.empty((k // 512, 16))
    for p in range(k // 512):
        a[p, :8] = np.random.permutation(np.resize(levels, 8))
        for g in range(8):
            far = levels[np.abs(levels - a[p, g]) >= 10]
            a[p, g + 8] = far[np.random.randint(len(far))]
    return np.exp2(a.ravel()).repeat(32)


def f64(x):
    return np.asarray(x).astype(np.float64)


def striped(idx):
    return np.tile(idx.reshape(-1, 16).T, (8, 1)).astype(np.uint16)


def unstriped(offs):
    return offs[:16].T.reshape(-1).astype(np.int64)


def pack_weight(w):
    k, n = w.shape
    w = f64(np.asarray(w, np.float32).astype(ml_dtypes.bfloat16)).reshape(k // 32, 32, n)
    amax = np.abs(w).max(1)
    byte = np.clip(np.where(amax > 0, np.frexp(amax)[1] - 1 + 127 - 7, 1), 1, 254)
    scaled = (w * np.exp2(127.0 - byte)[:, None, :]).reshape(k, n).astype(np.float32)
    words = np.ascontiguousarray(scaled.reshape(k // 512, 128, 4, n).transpose(0, 1, 3, 2)).astype(ml_dtypes.float8_e4m3fn).view(np.uint8)
    return words, np.ascontiguousarray(byte.astype(np.uint8).reshape(k // 512, 16, n))


def unpack_weight(words, scales):
    g, p, n, _ = words.shape
    vals = np.ascontiguousarray(words).view(ml_dtypes.float8_e4m3fn).astype(np.float64) * np.repeat(np.exp2(scales.astype(np.float64) - 127.0), 8, axis=1)[..., None]
    return vals.transpose(0, 1, 3, 2).reshape(g * 512, n)

def planes(y):
    n, m = y.shape
    v = y.astype(np.float32).astype(ml_dtypes.bfloat16).astype(np.float64).reshape(n // 32, 32, m)
    top = np.abs(v).max(1)
    byte = np.clip(np.where(top > 0, np.frexp(top)[1] - 1 + 127 - 7, 1), 1, 254)
    codes = (v * np.exp2(127.0 - byte)[:, None, :]).reshape(n, m).astype(np.float32).astype(ml_dtypes.float8_e4m3fn).view(np.uint8)
    words = codes.reshape(n // 512, 128, 4, m).transpose(0, 1, 3, 2)
    return np.ascontiguousarray(words), np.ascontiguousarray(byte.astype(np.uint8).reshape(n // 512, 16, m))


K, T, S, H = 512, 1024, 512, 512
P = 2 ** 7


def setup_inputs():
    n = np.random.standard_normal
    s = mx_kscale(K)[:, None]
    u = mx_kscale(H)
    packed_xT = pack_weight(n((K, T)) * s)
    packed_w2 = pack_weight(n((H, H)) / np.sqrt(H) / u[:, None])
    return {
        "x_words": packed_xT[0],
        "x_scales": packed_xT[1],
        "w1": (n((K, H)) / np.sqrt(K) / s * u).astype(np.float32),
        "w2_words": packed_w2[0],
        "w2_scales": packed_w2[1],
        "lam": np.tile(np.random.uniform(0.1, 0.9, S), (P, 1)).astype(np.float32),
        "mu": np.tile(np.random.uniform(0.1, 0.9, S), (P, 1)).astype(np.float32),
        "offs": striped(np.random.permutation(T)[:S]),
        "pos1": striped(np.random.permutation(S)),
    }


def reference(x_words, x_scales, w1, w2_words, w2_scales, lam, mu, offs, pos1):
    xq = unpack_weight(x_words, x_scales)[:, unstriped(offs)]
    h = mxq(f64(w1), 0, "e4m3").T @ xq
    z = h * f64(lam)[:1] + h[:, unstriped(pos1)] * f64(mu)[:1]
    out_0 = unpack_weight(w2_words, w2_scales).T @ mxq(z, 0, "e4m3")
    return (out_0,) + planes(out_0)

@@ -1,0 +1,205 @@
+from contextlib import ExitStack
+
+import concourse.mybir as mybir
+from concourse.masks import make_identity
+
+K, T, S, H = 512, 1024, 512, 512
+P = 128
+PACK = 4
+FLOPS = 2 * K * H * S + 2 * H * H * S
+
+F32 = mybir.dt.float32
+BF16 = mybir.dt.bfloat16
+I32 = mybir.dt.int32
+U32 = mybir.dt.uint32
+U16 = mybir.dt.uint16
+U8 = mybir.dt.uint8
+FP8X4 = mybir.dt.float8_e4m3fn_x4
+MULT = mybir.AluOpType.mult
+ADD = mybir.AluOpType.add
+COPY = mybir.ActivationFunctionType.Copy
+
+HALF = H // 2
+SCALAR_SHARE = 80
+GATHERS = [(0, 256), (256, 128), (384, 128)]
+BLOCKS = S // P
+
+
+def tile_picked_mixup_none_po_kernel(
+    tc, x_words, x_scales, w1, w2_words, w2_scales, lam, mu, offs, pos1, out_0, out_1, out_2
+):
+    nc = tc.nc
+    with ExitStack() as ctx:
+        keep = ctx.enter_context(tc.tile_pool(name="keep", bufs=1))
+        psum = ctx.enter_context(tc.psum_pool(name="psum", bufs=1))
+
+        def sb(name, shape, dtype, tag=None):
+            return keep.tile(shape, dtype, name=name, tag=tag or name, align_bytes=64)
+
+        def bank(name, shape, number):
+            return psum.tile(shape, F32, name=name, tag="bank%d" % number)
+
+        def load_scales(queues, tile, scales):
+            for q in range(4):
+                queues[q % len(queues)].dma_start(
+                    out=tile[32 * q : 32 * q + 32, :].bitcast(I32),
+                    in_=scales[0, 4 * q : 4 * q + 4, :].bitcast(I32).partition_broadcast(8),
+                )
+
+        offs_t = sb("offs_t", [P, S // 16], U16)
+        pos_t = sb("pos_t", [P, S // 16], U16)
+        xw = sb("xw", [P, T], I32)
+        xs = sb("xs", [P, T], U8)
+        w2w = sb("w2w", [P, H], I32)
+        w2s = sb("w2s", [P, H], U8)
+        lam_c = sb("lam_c", [P, BLOCKS], F32)
+        mu_t = sb("mu_t", [P, S], F32)
+        w1_raw = [sb("w1_raw%d" % c, [P, PACK, HALF], F32) for c in range(2)]
+        ident = sb("ident", [P, P], F32)
+        make_identity(nc, ident[:])
+
+        nc.sync.dma_start(offs_t[:], offs)
+        load_scales([nc.sync, nc.scalar], xs, x_scales)
+        nc.sync.dma_start(out=xw[:], in_=x_words[0].rearrange("p n t -> p (n t)").bitcast(I32))
+        w1_v = w1.rearrange("(p j) c -> p j c", j=PACK)
+        for c in range(2):
+            nc.sync.dma_start(out=w1_raw[c][:], in_=w1_v[:, :, c * HALF : (c + 1) * HALF])
+        nc.sync.dma_start(out=w2w[:], in_=w2_words[0].rearrange("p n t -> p (n t)").bitcast(I32))
+        nc.sync.dma_start(pos_t[:], pos1)
+        nc.sync.dma_start(out=mu_t[:], in_=mu)
+        load_scales([nc.sync], w2s, w2_scales)
+        with nc.allow_non_contiguous_dma(reason="one value a partition and block"):
+            nc.sync.dma_start(out=lam_c[:], in_=lam[0, :].rearrange("(c p) -> p c", p=P))
+
+        xqw = sb("xqw", [P, S], U32)
+        xqs = sb("xqs", [P, S], U8)
+        nc.vector.tensor_copy(xqs[:], xs[:].indirect(offs_t[:]))
+        nc.vector.tensor_copy(xqw[:], xw[:].bitcast(U32).indirect(offs_t[:]))
+
+        w1_bf = sb("w1_bf", [P, PACK, P, PACK], BF16)
+
+        def round_w1(copy, c0, c1):
+            half = c0 // HALF
+            src = w1_raw[half][:, :, c0 - half * HALF : c1 - half * HALF].rearrange("p j (m t) -> p m t j", t=PACK)
+            dst = w1_bf[:, :, c0 // PACK : c1 // PACK, :].rearrange("p t m j -> p m t j")
+            copy(out=dst, in_=src)
+
+        round_w1(nc.scalar.copy, 0, HALF)
+        round_w1(nc.scalar.copy, HALF, HALF + SCALAR_SHARE)
+        round_w1(nc.vector.tensor_copy, HALF + SCALAR_SHARE, H)
+        w1c = [sb("w1c%d" % t, [P, P], U32) for t in range(PACK)]
+        w1s = [sb("w1s%d" % t, [P, P], U8) for t in range(PACK)]
+        h = [sb("h%d" % t, [P, S], F32) for t in range(PACK)]
+        for t in range(PACK):
+            nc.vector.quantize_mx(
+                out=w1c[t][:].bitcast(FP8X4), scales=w1s[t][:], in_=w1_bf[:, t].rearrange("p m j -> p (m j)")
+            )
+            h_ps = bank("h_ps%d" % t, [P, S], t)
+            nc.tensor.matmul_mx(
+                out=h_ps[:], lhsT=w1c[t][:].bitcast(FP8X4), lhsT_scale=w1s[t][:],
+                rhs=xqw[:].bitcast(FP8X4), rhs_scale=xqs[:], start=True, stop=True,
+            )
+            nc.scalar.copy(out=h[t][:], in_=h_ps[:])
+
+        w2dw = sb("w2dw", [P, H], I32, tag="w1_bf")
+        w2ds = sb("w2ds", [P, H], U8, tag="w1s0")
+        nc.vector.tensor_copy(
+            out=w2dw[:].rearrange("p (t m) -> p m t", t=PACK), in_=w2w[:].rearrange("p (m t) -> p m t", t=PACK)
+        )
+        nc.vector.tensor_copy(
+            out=w2ds[:].rearrange("p (t m) -> p m t", t=PACK), in_=w2s[:].rearrange("p (m t) -> p m t", t=PACK)
+        )
+
+        own = []
+        turned = [bank("turned%d" % c, [P, PACK, P], PACK + c) for c in range(BLOCKS)]
+        for t in range(PACK):
+            for c in range(BLOCKS):
+                nc.tensor.transpose(turned[c][:, t, :], h[t][:, c * P : (c + 1) * P], ident[:])
+        for c in range(BLOCKS):
+            scaled = sb("scaled%d" % c, [P, PACK, P], F32)
+            nc.scalar.activation(out=scaled[:], in_=turned[c][:], func=COPY, scale=lam_c[:, c : c + 1])
+            own_c = bank("own%d" % c, [P, PACK, P], c)
+            for t in range(PACK):
+                nc.tensor.transpose(own_c[:, t, :], scaled[:, t, :], ident[:])
+            own.append(own_c)
+
+        oc = sb("oc", [P, S], I32)
+        osc = sb("osc", [P, S], U8)
+        out0_v = out_0.rearrange("(p t) j -> p t j", t=PACK)
+        out1_v = out_1[0].rearrange("p n t -> p (n t)").bitcast(I32)
+        partner = {}
+
+        def gathers(i):
+            j0, w = GATHERS[i]
+            g = sb("g%d" % i, [P, PACK, w], F32)
+            for t in range(PACK):
+                nc.vector.tensor_tensor(
+                    g[:, t, :], h[t][:].indirect(pos_t[:, j0 // 16 : (j0 + w) // 16]), mu_t[:, j0 : j0 + w], MULT
+                )
+            for s0 in range(0, w, P):
+                partner[(j0 + s0) // P] = g[:, :, s0 : s0 + P]
+
+        def mix(c):
+            z = sb("z%d" % c, [P, P * PACK], BF16)
+            nc.vector.tensor_tensor(
+                z[:].rearrange("p (c i t) -> p c t i", i=4, t=PACK),
+                own[c][:].rearrange("p t (c i) -> p c t i", i=4),
+                partner[c].rearrange("p t (c i) -> p c t i", i=4),
+                ADD,
+            )
+            return z
+
+        def second(c, z):
+            j = c * P
+            zc = sb("zc%d" % c, [P, P], U32)
+            zs = sb("zs%d" % c, [P, P], U8)
+            nc.vector.quantize_mx(out=zc[:].bitcast(FP8X4), scales=zs[:], in_=z[:])
+            y_ps = bank("y_ps%d" % c, [P, PACK, P], PACK + c)
+            for t in range(PACK):
+                nc.tensor.matmul_mx(
+                    out=y_ps[:, t, :],
+                    lhsT=w2dw[:, t * P : (t + 1) * P].bitcast(FP8X4), lhsT_scale=w2ds[:, t * P : (t + 1) * P],
+                    rhs=zc[:].bitcast(FP8X4), rhs_scale=zs[:],
+                    start=True, stop=True,
+                )
+            y = sb("y%d" % c, [P, PACK, P], F32)
+            yb = sb("yb%d" % c, [P, P, PACK], BF16)
+            nc.scalar.copy(out=y[:], in_=y_ps[:])
+            nc.sync.dma_start(out=out0_v[:, :, j : j + P], in_=y[:])
+            if c < 2:
+                nc.scalar.copy(out=yb[:], in_=y_ps[:].rearrange("p t j -> p j t"))
+            else:
+                nc.vector.tensor_copy(
+                    out=yb[:].rearrange("p (c i) t -> p c t i", i=4),
+                    in_=y[:].rearrange("p t (c i) -> p c t i", i=4),
+                )
+            return yb
+
+        def planes(c, yb):
+            j = c * P
+            nc.vector.quantize_mx(
+                out=oc[:, j : j + P].bitcast(FP8X4), scales=osc[:, j : j + P],
+                in_=yb[:].rearrange("p j t -> p (j t)"),
+            )
+            nc.sync.dma_start(out=out1_v[:, j : j + P], in_=oc[:, j : j + P])
+
+        gathers(0)
+        gathers(1)
+        z0 = mix(0)
+        z1 = mix(1)
+        y0 = second(0, z0)
+        z2 = mix(2)
+        y1 = second(1, z1)
+        y2 = second(2, z2)
+        gathers(2)
+        z3 = mix(3)
+        y3 = second(3, z3)
+        planes(0, y0)
+        planes(1, y1)
+        planes(2, y2)
+        planes(3, y3)
+        for q in range(4):
+            queue = nc.sync if q % 2 == 0 else nc.scalar
+            queue.dma_start(
+                out=out_2[0, 4 * q : 4 * q + 4, :].bitcast(I32), in_=osc[32 * q : 32 * q + 4, :].bitcast(I32)
+            )

@@ -21,7 +21,7 @@ COPY = mybir.ActivationFunctionType.Copy
 
 HALF = H // 2
 SCALAR_SHARE = 80
-GATHERS = [(0, 256), (256, 128), (384, 128)]
+GATHER_W = 256
 BLOCKS = S // P
 
 
@@ -31,6 +31,7 @@ def tile_picked_mixup_none_po_kernel(
     nc = tc.nc
     with ExitStack() as ctx:
         keep = ctx.enter_context(tc.tile_pool(name="keep", bufs=1))
+        early = ctx.enter_context(tc.tile_pool(name="early", bufs=1))
         psum = ctx.enter_context(tc.psum_pool(name="psum", bufs=1))
 
         def sb(name, shape, dtype, tag=None):
@@ -42,46 +43,49 @@ def tile_picked_mixup_none_po_kernel(
         def load_scales(queues, tile, scales):
             for q in range(4):
                 queues[q % len(queues)].dma_start(
-                    out=tile[32 * q : 32 * q + 32, :].bitcast(I32),
-                    in_=scales[0, 4 * q : 4 * q + 4, :].bitcast(I32).partition_broadcast(8),
+                    out=tile[32 * q : 32 * q + 4, :].bitcast(I32),
+                    in_=scales[0, 4 * q : 4 * q + 4, :].bitcast(I32),
                 )
 
         offs_t = sb("offs_t", [P, S // 16], U16)
         pos_t = sb("pos_t", [P, S // 16], U16)
-        xw = sb("xw", [P, T], I32)
+        xw = early.tile([P, T], I32, name="xw", offset=1024)
         xs = sb("xs", [P, T], U8)
-        w2w = sb("w2w", [P, H], I32)
-        w2s = sb("w2s", [P, H], U8)
-        lam_c = sb("lam_c", [P, BLOCKS], F32)
-        mu_t = sb("mu_t", [P, S], F32)
         w1_raw = [sb("w1_raw%d" % c, [P, PACK, HALF], F32) for c in range(2)]
+        nc.vector.memset(xs[:].bitcast(I32), 0)
         ident = sb("ident", [P, P], F32)
         make_identity(nc, ident[:])
 
         nc.sync.dma_start(offs_t[:], offs)
-        load_scales([nc.sync, nc.scalar], xs, x_scales)
+        load_scales([nc.scalar], xs, x_scales)
         nc.sync.dma_start(out=xw[:], in_=x_words[0].rearrange("p n t -> p (n t)").bitcast(I32))
         w1_v = w1.rearrange("(p j) c -> p j c", j=PACK)
         for c in range(2):
             nc.sync.dma_start(out=w1_raw[c][:], in_=w1_v[:, :, c * HALF : (c + 1) * HALF])
-        nc.sync.dma_start(out=w2w[:], in_=w2_words[0].rearrange("p n t -> p (n t)").bitcast(I32))
         nc.sync.dma_start(pos_t[:], pos1)
+
+        xqw = sb("xqw", [P, S], U32)
+        xqs = sb("xqs", [P, S], U8)
+        nc.vector.tensor_copy(xqw[:], xw[:].bitcast(U32).indirect(offs_t[:]))
+        nc.vector.tensor_copy(xqs[:], xs[:].indirect(offs_t[:]))
+
+        mu_t = early.tile([P, S], F32, name="mu_t", offset=0)
+        w2s = early.tile([P, H], U8, name="w2s", offset=2048)
+        lam_c = early.tile([P, BLOCKS], F32, name="lam_c", offset=2560)
+        w2w = early.tile([P, H], I32, name="w2w", offset=3072)
+        nc.gpsimd.memset(w2s[:].bitcast(I32), 0)
+        nc.sync.dma_start(out=w2w[:], in_=w2_words[0].rearrange("p n t -> p (n t)").bitcast(I32))
         nc.sync.dma_start(out=mu_t[:], in_=mu)
         load_scales([nc.sync], w2s, w2_scales)
         with nc.allow_non_contiguous_dma(reason="one value a partition and block"):
             nc.sync.dma_start(out=lam_c[:], in_=lam[0, :].rearrange("(c p) -> p c", p=P))
 
-        xqw = sb("xqw", [P, S], U32)
-        xqs = sb("xqs", [P, S], U8)
-        nc.vector.tensor_copy(xqs[:], xs[:].indirect(offs_t[:]))
-        nc.vector.tensor_copy(xqw[:], xw[:].bitcast(U32).indirect(offs_t[:]))
-
         w1_bf = sb("w1_bf", [P, PACK, P, PACK], BF16)
 
         def round_w1(copy, c0, c1):
             half = c0 // HALF
-            src = w1_raw[half][:, :, c0 - half * HALF : c1 - half * HALF].rearrange("p j (m t) -> p m t j", t=PACK)
-            dst = w1_bf[:, :, c0 // PACK : c1 // PACK, :].rearrange("p t m j -> p m t j")
+            src = w1_raw[half][:, :, c0 - half * HALF : c1 - half * HALF].rearrange("p j (m u e) -> p u m j e", u=2, e=2)
+            dst = w1_bf[:, :, c0 // PACK : c1 // PACK, :].rearrange("p (u e) m j -> p u m j e", e=2)
             copy(out=dst, in_=src)
 
         round_w1(nc.scalar.copy, 0, HALF)
@@ -104,16 +108,17 @@ def tile_picked_mixup_none_po_kernel(
         w2dw = sb("w2dw", [P, H], I32, tag="w1_bf")
         w2ds = sb("w2ds", [P, H], U8, tag="w1s0")
         nc.vector.tensor_copy(
-            out=w2dw[:].rearrange("p (t m) -> p m t", t=PACK), in_=w2w[:].rearrange("p (m t) -> p m t", t=PACK)
+            out=w2dw[:].rearrange("p (u e m) -> p u m e", u=2, e=2),
+            in_=w2w[:].rearrange("p (m u e) -> p u m e", u=2, e=2),
         )
         nc.vector.tensor_copy(
-            out=w2ds[:].rearrange("p (t m) -> p m t", t=PACK), in_=w2s[:].rearrange("p (m t) -> p m t", t=PACK)
+            out=w2ds[:].rearrange("p (t m) -> p t m", t=PACK), in_=w2s[:].rearrange("p (m t) -> p t m", t=PACK)
         )
 
         own = []
         turned = [bank("turned%d" % c, [P, PACK, P], PACK + c) for c in range(BLOCKS)]
-        for t in range(PACK):
-            for c in range(BLOCKS):
+        for c in range(BLOCKS):
+            for t in range(PACK):
                 nc.tensor.transpose(turned[c][:, t, :], h[t][:, c * P : (c + 1) * P], ident[:])
         for c in range(BLOCKS):
             scaled = sb("scaled%d" % c, [P, PACK, P], F32)
@@ -127,30 +132,27 @@ def tile_picked_mixup_none_po_kernel(
         osc = sb("osc", [P, S], U8)
         out0_v = out_0.rearrange("(p t) j -> p t j", t=PACK)
         out1_v = out_1[0].rearrange("p n t -> p (n t)").bitcast(I32)
-        partner = {}
-
-        def gathers(i):
-            j0, w = GATHERS[i]
-            g = sb("g%d" % i, [P, PACK, w], F32)
-            for t in range(PACK):
+        partner = sb("partner", [P, PACK, S], F32)
+        for t in range(PACK):
+            for j0 in range(0, S, GATHER_W):
                 nc.vector.tensor_tensor(
-                    g[:, t, :], h[t][:].indirect(pos_t[:, j0 // 16 : (j0 + w) // 16]), mu_t[:, j0 : j0 + w], MULT
+                    partner[:, t, j0 : j0 + GATHER_W],
+                    h[t][:].indirect(pos_t[:, j0 // 16 : (j0 + GATHER_W) // 16]),
+                    mu_t[:, j0 : j0 + GATHER_W],
+                    MULT,
                 )
-            for s0 in range(0, w, P):
-                partner[(j0 + s0) // P] = g[:, :, s0 : s0 + P]
 
         def mix(c):
             z = sb("z%d" % c, [P, P * PACK], BF16)
             nc.vector.tensor_tensor(
-                z[:].rearrange("p (c i t) -> p c t i", i=4, t=PACK),
-                own[c][:].rearrange("p t (c i) -> p c t i", i=4),
-                partner[c].rearrange("p t (c i) -> p c t i", i=4),
+                z[:].rearrange("p (c i t) -> p c t i", i=2, t=PACK),
+                own[c][:].rearrange("p t (c i) -> p c t i", i=2),
+                partner[:, :, c * P : (c + 1) * P].rearrange("p t (c i) -> p c t i", i=2),
                 ADD,
             )
             return z
 
         def second(c, z):
-            j = c * P
             zc = sb("zc%d" % c, [P, P], U32)
             zs = sb("zs%d" % c, [P, P], U8)
             nc.vector.quantize_mx(out=zc[:].bitcast(FP8X4), scales=zs[:], in_=z[:])
@@ -162,17 +164,19 @@ def tile_picked_mixup_none_po_kernel(
                     rhs=zc[:].bitcast(FP8X4), rhs_scale=zs[:],
                     start=True, stop=True,
                 )
+            return y_ps
+
+        def way_out(c, y_ps):
+            j = c * P
             y = sb("y%d" % c, [P, PACK, P], F32)
             yb = sb("yb%d" % c, [P, P, PACK], BF16)
             nc.scalar.copy(out=y[:], in_=y_ps[:])
-            nc.sync.dma_start(out=out0_v[:, :, j : j + P], in_=y[:])
-            if c < 2:
-                nc.scalar.copy(out=yb[:], in_=y_ps[:].rearrange("p t j -> p j t"))
-            else:
-                nc.vector.tensor_copy(
-                    out=yb[:].rearrange("p (c i) t -> p c t i", i=4),
-                    in_=y[:].rearrange("p t (c i) -> p c t i", i=4),
-                )
+            queue = nc.sync if c < BLOCKS - 1 else nc.scalar
+            queue.dma_start(out=out0_v[:, :, j : j + P], in_=y[:])
+            nc.vector.tensor_copy(
+                out=yb[:].rearrange("p (c i) t -> p c t i", i=2),
+                in_=y[:].rearrange("p t (c i) -> p c t i", i=2),
+            )
             return yb
 
         def planes(c, yb):
@@ -181,25 +185,23 @@ def tile_picked_mixup_none_po_kernel(
                 out=oc[:, j : j + P].bitcast(FP8X4), scales=osc[:, j : j + P],
                 in_=yb[:].rearrange("p j t -> p (j t)"),
             )
-            nc.sync.dma_start(out=out1_v[:, j : j + P], in_=oc[:, j : j + P])
+            if c >= BLOCKS - 2:
+                j0 = 0 if c == BLOCKS - 2 else j
+                nc.sync.dma_start(out=out1_v[:, j0 : j + P], in_=oc[:, j0 : j + P])
 
-        gathers(0)
-        gathers(1)
-        z0 = mix(0)
-        z1 = mix(1)
-        y0 = second(0, z0)
-        z2 = mix(2)
-        y1 = second(1, z1)
-        y2 = second(2, z2)
-        gathers(2)
-        z3 = mix(3)
-        y3 = second(3, z3)
-        planes(0, y0)
-        planes(1, y1)
-        planes(2, y2)
-        planes(3, y3)
+        z = [mix(0)]
+        y_ps = []
+        for c in range(BLOCKS):
+            if c + 1 < BLOCKS:
+                z.append(mix(c + 1))
+            y_ps.append(second(c, z[c]))
+        yb = [way_out(0, y_ps[0])]
+        for c in range(BLOCKS):
+            if c + 1 < BLOCKS:
+                yb.append(way_out(c + 1, y_ps[c + 1]))
+            planes(c, yb[c])
         for q in range(4):
-            queue = nc.sync if q % 2 == 0 else nc.scalar
+            queue = nc.sync if q < 2 else nc.scalar
             queue.dma_start(
                 out=out_2[0, 4 * q : 4 * q + 4, :].bitcast(I32), in_=osc[32 * q : 32 * q + 4, :].bitcast(I32)
             )

@@ -31,7 +31,6 @@ def tile_picked_mixup_none_po_kernel(
     nc = tc.nc
     with ExitStack() as ctx:
         keep = ctx.enter_context(tc.tile_pool(name="keep", bufs=1))
-        early = ctx.enter_context(tc.tile_pool(name="early", bufs=1))
         psum = ctx.enter_context(tc.psum_pool(name="psum", bufs=1))
 
         def sb(name, shape, dtype, tag=None):
@@ -43,49 +42,46 @@ def tile_picked_mixup_none_po_kernel(
         def load_scales(queues, tile, scales):
             for q in range(4):
                 queues[q % len(queues)].dma_start(
-                    out=tile[32 * q : 32 * q + 4, :].bitcast(I32),
-                    in_=scales[0, 4 * q : 4 * q + 4, :].bitcast(I32),
+                    out=tile[32 * q : 32 * q + 32, :].bitcast(I32),
+                    in_=scales[0, 4 * q : 4 * q + 4, :].bitcast(I32).partition_broadcast(8),
                 )
 
         offs_t = sb("offs_t", [P, S // 16], U16)
         pos_t = sb("pos_t", [P, S // 16], U16)
-        xw = early.tile([P, T], I32, name="xw", offset=1024)
+        xw = sb("xw", [P, T], I32)
+        w2w = sb("w2w", [P, H], I32)
+        w2s = sb("w2s", [P, H], U8)
+        lam_c = sb("lam_c", [P, BLOCKS], F32)
+        mu_t = sb("mu_t", [P, S], F32)
         xs = sb("xs", [P, T], U8)
         w1_raw = [sb("w1_raw%d" % c, [P, PACK, HALF], F32) for c in range(2)]
-        nc.vector.memset(xs[:].bitcast(I32), 0)
         ident = sb("ident", [P, P], F32)
         make_identity(nc, ident[:])
 
         nc.sync.dma_start(offs_t[:], offs)
-        load_scales([nc.scalar], xs, x_scales)
+        load_scales([nc.sync], xs, x_scales)
         nc.sync.dma_start(out=xw[:], in_=x_words[0].rearrange("p n t -> p (n t)").bitcast(I32))
         w1_v = w1.rearrange("(p j) c -> p j c", j=PACK)
         for c in range(2):
             nc.sync.dma_start(out=w1_raw[c][:], in_=w1_v[:, :, c * HALF : (c + 1) * HALF])
+        nc.sync.dma_start(out=w2w[:], in_=w2_words[0].rearrange("p n t -> p (n t)").bitcast(I32))
+        load_scales([nc.sync], w2s, w2_scales)
         nc.sync.dma_start(pos_t[:], pos1)
+        nc.sync.dma_start(out=mu_t[:], in_=mu)
+        with nc.allow_non_contiguous_dma(reason="one value a partition and block"):
+            nc.sync.dma_start(out=lam_c[:], in_=lam[0, :].rearrange("(c p) -> p c", p=P))
 
         xqw = sb("xqw", [P, S], U32)
         xqs = sb("xqs", [P, S], U8)
-        nc.vector.tensor_copy(xqw[:], xw[:].bitcast(U32).indirect(offs_t[:]))
         nc.vector.tensor_copy(xqs[:], xs[:].indirect(offs_t[:]))
-
-        mu_t = early.tile([P, S], F32, name="mu_t", offset=0)
-        w2s = early.tile([P, H], U8, name="w2s", offset=2048)
-        lam_c = early.tile([P, BLOCKS], F32, name="lam_c", offset=2560)
-        w2w = early.tile([P, H], I32, name="w2w", offset=3072)
-        nc.gpsimd.memset(w2s[:].bitcast(I32), 0)
-        nc.sync.dma_start(out=w2w[:], in_=w2_words[0].rearrange("p n t -> p (n t)").bitcast(I32))
-        nc.sync.dma_start(out=mu_t[:], in_=mu)
-        load_scales([nc.sync], w2s, w2_scales)
-        with nc.allow_non_contiguous_dma(reason="one value a partition and block"):
-            nc.sync.dma_start(out=lam_c[:], in_=lam[0, :].rearrange("(c p) -> p c", p=P))
+        nc.vector.tensor_copy(xqw[:], xw[:].bitcast(U32).indirect(offs_t[:]))
 
         w1_bf = sb("w1_bf", [P, PACK, P, PACK], BF16)
 
         def round_w1(copy, c0, c1):
             half = c0 // HALF
-            src = w1_raw[half][:, :, c0 - half * HALF : c1 - half * HALF].rearrange("p j (m u e) -> p u m j e", u=2, e=2)
-            dst = w1_bf[:, :, c0 // PACK : c1 // PACK, :].rearrange("p (u e) m j -> p u m j e", e=2)
+            src = w1_raw[half][:, :, c0 - half * HALF : c1 - half * HALF].rearrange("p j (m t) -> p m t j", t=PACK)
+            dst = w1_bf[:, :, c0 // PACK : c1 // PACK, :].rearrange("p t m j -> p m t j")
             copy(out=dst, in_=src)
 
         round_w1(nc.scalar.copy, 0, HALF)
@@ -98,18 +94,21 @@ def tile_picked_mixup_none_po_kernel(
             nc.vector.quantize_mx(
                 out=w1c[t][:].bitcast(FP8X4), scales=w1s[t][:], in_=w1_bf[:, t].rearrange("p m j -> p (m j)")
             )
-            h_ps = bank("h_ps%d" % t, [P, S], t)
-            nc.tensor.matmul_mx(
-                out=h_ps[:], lhsT=w1c[t][:].bitcast(FP8X4), lhsT_scale=w1s[t][:],
-                rhs=xqw[:].bitcast(FP8X4), rhs_scale=xqs[:], start=True, stop=True,
-            )
-            nc.scalar.copy(out=h[t][:], in_=h_ps[:])
+            banks = [0, PACK] if t == 0 else [t]
+            width = S // len(banks)
+            for i, number in enumerate(banks):
+                cols = slice(i * width, (i + 1) * width)
+                h_ps = bank("h_ps%d_%d" % (t, i), [P, width], number)
+                nc.tensor.matmul_mx(
+                    out=h_ps[:], lhsT=w1c[t][:].bitcast(FP8X4), lhsT_scale=w1s[t][:],
+                    rhs=xqw[:, cols].bitcast(FP8X4), rhs_scale=xqs[:, cols], start=True, stop=True,
+                )
+                nc.scalar.copy(out=h[t][:, cols], in_=h_ps[:])
 
         w2dw = sb("w2dw", [P, H], I32, tag="w1_bf")
         w2ds = sb("w2ds", [P, H], U8, tag="w1s0")
         nc.vector.tensor_copy(
-            out=w2dw[:].rearrange("p (u e m) -> p u m e", u=2, e=2),
-            in_=w2w[:].rearrange("p (m u e) -> p u m e", u=2, e=2),
+            out=w2dw[:].rearrange("p (t m) -> p m t", t=PACK), in_=w2w[:].rearrange("p (m t) -> p m t", t=PACK)
         )
         nc.vector.tensor_copy(
             out=w2ds[:].rearrange("p (t m) -> p t m", t=PACK), in_=w2s[:].rearrange("p (m t) -> p t m", t=PACK)
@@ -145,9 +144,9 @@ def tile_picked_mixup_none_po_kernel(
         def mix(c):
             z = sb("z%d" % c, [P, P * PACK], BF16)
             nc.vector.tensor_tensor(
-                z[:].rearrange("p (c i t) -> p c t i", i=2, t=PACK),
-                own[c][:].rearrange("p t (c i) -> p c t i", i=2),
-                partner[:, :, c * P : (c + 1) * P].rearrange("p t (c i) -> p c t i", i=2),
+                z[:].rearrange("p (j t) -> p j t", t=PACK),
+                own[c][:].rearrange("p t j -> p j t"),
+                partner[:, :, c * P : (c + 1) * P].rearrange("p t j -> p j t"),
                 ADD,
             )
             return z
@@ -156,10 +155,14 @@ def tile_picked_mixup_none_po_kernel(
             zc = sb("zc%d" % c, [P, P], U32)
             zs = sb("zs%d" % c, [P, P], U8)
             nc.vector.quantize_mx(out=zc[:].bitcast(FP8X4), scales=zs[:], in_=z[:])
-            y_ps = bank("y_ps%d" % c, [P, PACK, P], PACK + c)
+            if c < BLOCKS - 1:
+                y_ps = [bank("y_ps%d" % c, [P, PACK, P], PACK + c)]
+            else:
+                y_ps = [bank("y_ps%d_%d" % (c, t), [P, 1, P], (PACK + c + t) % 8) for t in range(PACK)]
+            rows = PACK // len(y_ps)
             for t in range(PACK):
                 nc.tensor.matmul_mx(
-                    out=y_ps[:, t, :],
+                    out=y_ps[t // rows][:, t % rows, :],
                     lhsT=w2dw[:, t * P : (t + 1) * P].bitcast(FP8X4), lhsT_scale=w2ds[:, t * P : (t + 1) * P],
                     rhs=zc[:].bitcast(FP8X4), rhs_scale=zs[:],
                     start=True, stop=True,
@@ -170,13 +173,12 @@ def tile_picked_mixup_none_po_kernel(
             j = c * P
             y = sb("y%d" % c, [P, PACK, P], F32)
             yb = sb("yb%d" % c, [P, P, PACK], BF16)
-            nc.scalar.copy(out=y[:], in_=y_ps[:])
+            rows = PACK // len(y_ps)
+            for i, part in enumerate(y_ps):
+                nc.scalar.copy(out=y[:, i * rows : (i + 1) * rows, :], in_=part[:])
             queue = nc.sync if c < BLOCKS - 1 else nc.scalar
             queue.dma_start(out=out0_v[:, :, j : j + P], in_=y[:])
-            nc.vector.tensor_copy(
-                out=yb[:].rearrange("p (c i) t -> p c t i", i=2),
-                in_=y[:].rearrange("p t (c i) -> p c t i", i=2),
-            )
+            nc.vector.tensor_copy(out=yb[:], in_=y[:].rearrange("p t j -> p j t"))
             return yb
 
         def planes(c, yb):

@@ -20,7 +20,7 @@ ADD = mybir.AluOpType.add
 COPY = mybir.ActivationFunctionType.Copy
 
 HALF = H // 2
-SCALAR_SHARE = 80
+SCALAR_SHARE = 64
 GATHER_W = 256
 BLOCKS = S // P
 
@@ -31,6 +31,7 @@ def tile_picked_mixup_none_po_kernel(
     nc = tc.nc
     with ExitStack() as ctx:
         keep = ctx.enter_context(tc.tile_pool(name="keep", bufs=1))
+        shared = ctx.enter_context(tc.tile_pool(name="shared", bufs=1))
         psum = ctx.enter_context(tc.psum_pool(name="psum", bufs=1))
 
         def sb(name, shape, dtype, tag=None):
@@ -57,10 +58,13 @@ def tile_picked_mixup_none_po_kernel(
         w1_raw = [sb("w1_raw%d" % c, [P, PACK, HALF], F32) for c in range(2)]
         ident = sb("ident", [P, P], F32)
         make_identity(nc, ident[:])
+        lam_r = sb("lam_r", [P, P], F32)
+        nc.gpsimd.memset(lam_r[:], 0.0)
+        nc.gpsimd.dma_start(out=lam_r[0:BLOCKS, :], in_=lam[0, :].rearrange("(c j) -> c j", j=P))
 
+        nc.sync.dma_start(out=xw[:], in_=x_words[0].rearrange("p n t -> p (n t)").bitcast(I32))
         nc.sync.dma_start(offs_t[:], offs)
         load_scales([nc.sync], xs, x_scales)
-        nc.sync.dma_start(out=xw[:], in_=x_words[0].rearrange("p n t -> p (n t)").bitcast(I32))
         w1_v = w1.rearrange("(p j) c -> p j c", j=PACK)
         for c in range(2):
             nc.sync.dma_start(out=w1_raw[c][:], in_=w1_v[:, :, c * HALF : (c + 1) * HALF])
@@ -68,15 +72,13 @@ def tile_picked_mixup_none_po_kernel(
         load_scales([nc.sync], w2s, w2_scales)
         nc.sync.dma_start(pos_t[:], pos1)
         nc.sync.dma_start(out=mu_t[:], in_=mu)
-        with nc.allow_non_contiguous_dma(reason="one value a partition and block"):
-            nc.sync.dma_start(out=lam_c[:], in_=lam[0, :].rearrange("(c p) -> p c", p=P))
 
         xqw = sb("xqw", [P, S], U32)
         xqs = sb("xqs", [P, S], U8)
-        nc.vector.tensor_copy(xqs[:], xs[:].indirect(offs_t[:]))
         nc.vector.tensor_copy(xqw[:], xw[:].bitcast(U32).indirect(offs_t[:]))
+        nc.vector.tensor_copy(xqs[:], xs[:].indirect(offs_t[:]))
 
-        w1_bf = sb("w1_bf", [P, PACK, P, PACK], BF16)
+        w1_bf = shared.tile([P, PACK, P, PACK], BF16, name="w1_bf", align_bytes=64, offset=0)
 
         def round_w1(copy, c0, c1):
             half = c0 // HALF
@@ -87,6 +89,9 @@ def tile_picked_mixup_none_po_kernel(
         round_w1(nc.scalar.copy, 0, HALF)
         round_w1(nc.scalar.copy, HALF, HALF + SCALAR_SHARE)
         round_w1(nc.vector.tensor_copy, HALF + SCALAR_SHARE, H)
+        lam_ps = bank("lam_ps", [P, P], 7)
+        nc.tensor.transpose(lam_ps[:], lam_r[:], ident[:])
+        nc.scalar.copy(out=lam_c[:], in_=lam_ps[:, 0:BLOCKS])
         w1c = [sb("w1c%d" % t, [P, P], U32) for t in range(PACK)]
         w1s = [sb("w1s%d" % t, [P, P], U8) for t in range(PACK)]
         h = [sb("h%d" % t, [P, S], F32) for t in range(PACK)]
@@ -105,8 +110,8 @@ def tile_picked_mixup_none_po_kernel(
                 )
                 nc.scalar.copy(out=h[t][:, cols], in_=h_ps[:])
 
-        w2dw = sb("w2dw", [P, H], I32, tag="w1_bf")
-        w2ds = sb("w2ds", [P, H], U8, tag="w1s0")
+        w2dw = shared.tile([P, H], I32, name="w2dw", align_bytes=64, offset=0)
+        w2ds = shared.tile([P, H], U8, name="w2ds", align_bytes=64, offset=4 * H)
         nc.vector.tensor_copy(
             out=w2dw[:].rearrange("p (t m) -> p m t", t=PACK), in_=w2w[:].rearrange("p (m t) -> p m t", t=PACK)
         )

@@ -82,8 +82,8 @@ def tile_picked_mixup_none_po_kernel(
 
         def round_w1(copy, c0, c1):
             half = c0 // HALF
-            src = w1_raw[half][:, :, c0 - half * HALF : c1 - half * HALF].rearrange("p j (m t) -> p m t j", t=PACK)
-            dst = w1_bf[:, :, c0 // PACK : c1 // PACK, :].rearrange("p t m j -> p m t j")
+            src = w1_raw[half][:, :, c0 - half * HALF : c1 - half * HALF].rearrange("p j (m u e) -> p m u j e", u=2, e=2)
+            dst = w1_bf[:, :, c0 // PACK : c1 // PACK, :].rearrange("p (u e) m j -> p m u j e", e=2)
             copy(out=dst, in_=src)
 
         round_w1(nc.scalar.copy, 0, HALF)
@@ -149,9 +149,9 @@ def tile_picked_mixup_none_po_kernel(
         def mix(c):
             z = sb("z%d" % c, [P, P * PACK], BF16)
             nc.vector.tensor_tensor(
-                z[:].rearrange("p (j t) -> p j t", t=PACK),
-                own[c][:].rearrange("p t j -> p j t"),
-                partner[:, :, c * P : (c + 1) * P].rearrange("p t j -> p j t"),
+                z[:].rearrange("p (j e t) -> p j t e", e=2, t=PACK),
+                own[c][:].rearrange("p t (j e) -> p j t e", e=2),
+                partner[:, :, c * P : (c + 1) * P].rearrange("p t (j e) -> p j t e", e=2),
                 ADD,
             )
             return z
@@ -183,7 +183,9 @@ def tile_picked_mixup_none_po_kernel(
                 nc.scalar.copy(out=y[:, i * rows : (i + 1) * rows, :], in_=part[:])
             queue = nc.sync if c < BLOCKS - 1 else nc.scalar
             queue.dma_start(out=out0_v[:, :, j : j + P], in_=y[:])
-            nc.vector.tensor_copy(out=yb[:], in_=y[:].rearrange("p t j -> p j t"))
+            nc.vector.tensor_copy(
+                out=yb[:].rearrange("p (j e) t -> p j t e", e=2), in_=y[:].rearrange("p t (j e) -> p j t e", e=2)
+            )
             return yb
 
         def planes(c, yb):

@@ -43,8 +43,7 @@ def tile_picked_mixup_none_po_kernel(
         def load_scales(queues, tile, scales):
             for q in range(4):
                 queues[q % len(queues)].dma_start(
-                    out=tile[32 * q : 32 * q + 32, :].bitcast(I32),
-                    in_=scales[0, 4 * q : 4 * q + 4, :].bitcast(I32).partition_broadcast(8),
+                    out=tile[32 * q : 32 * q + 4, :].bitcast(I32), in_=scales[0, 4 * q : 4 * q + 4, :].bitcast(I32)
                 )
 
         offs_t = sb("offs_t", [P, S // 16], U16)
@@ -57,10 +56,9 @@ def tile_picked_mixup_none_po_kernel(
         xs = sb("xs", [P, T], U8)
         w1_raw = [sb("w1_raw%d" % c, [P, PACK, HALF], F32) for c in range(2)]
         ident = sb("ident", [P, P], F32)
+        nc.gpsimd.memset(xs[:].bitcast(I32), 0)
+        nc.vector.memset(w2s[:].bitcast(I32), 0)
         make_identity(nc, ident[:])
-        lam_r = sb("lam_r", [P, P], F32)
-        nc.gpsimd.memset(lam_r[:], 0.0)
-        nc.gpsimd.dma_start(out=lam_r[0:BLOCKS, :], in_=lam[0, :].rearrange("(c j) -> c j", j=P))
 
         nc.sync.dma_start(out=xw[:], in_=x_words[0].rearrange("p n t -> p (n t)").bitcast(I32))
         nc.sync.dma_start(offs_t[:], offs)
@@ -72,6 +70,8 @@ def tile_picked_mixup_none_po_kernel(
         load_scales([nc.sync], w2s, w2_scales)
         nc.sync.dma_start(pos_t[:], pos1)
         nc.sync.dma_start(out=mu_t[:], in_=mu)
+        with nc.allow_non_contiguous_dma(reason="one value of lam for each partition and block"):
+            nc.sync.dma_start(out=lam_c[:], in_=lam[0, :].rearrange("(c p) -> p c", p=P))
 
         xqw = sb("xqw", [P, S], U32)
         xqs = sb("xqs", [P, S], U8)
@@ -89,9 +89,6 @@ def tile_picked_mixup_none_po_kernel(
         round_w1(nc.scalar.copy, 0, HALF)
         round_w1(nc.scalar.copy, HALF, HALF + SCALAR_SHARE)
         round_w1(nc.vector.tensor_copy, HALF + SCALAR_SHARE, H)
-        lam_ps = bank("lam_ps", [P, P], 7)
-        nc.tensor.transpose(lam_ps[:], lam_r[:], ident[:])
-        nc.scalar.copy(out=lam_c[:], in_=lam_ps[:, 0:BLOCKS])
         w1c = [sb("w1c%d" % t, [P, P], U32) for t in range(PACK)]
         w1s = [sb("w1s%d" % t, [P, P], U8) for t in range(PACK)]
         h = [sb("h%d" % t, [P, S], F32) for t in range(PACK)]

@@ -20,9 +20,11 @@ ADD = mybir.AluOpType.add
 COPY = mybir.ActivationFunctionType.Copy
 
 HALF = H // 2
-SCALAR_SHARE = 64
-GATHER_W = 256
 BLOCKS = S // P
+FIRST_BANKS = ((0, 4), (1,), (2,), (3, 7))
+TURN_BANKS = (5, 6, 3, 7)
+OWN_BANKS = (0, 1, 2, 4)
+OUT_BANKS = ((5,), (6,), (3,), (7, 0, 1, 2))
 
 
 def tile_picked_mixup_none_po_kernel(
@@ -80,15 +82,14 @@ def tile_picked_mixup_none_po_kernel(
 
         w1_bf = shared.tile([P, PACK, P, PACK], BF16, name="w1_bf", align_bytes=64, offset=0)
 
-        def round_w1(copy, c0, c1):
-            half = c0 // HALF
-            src = w1_raw[half][:, :, c0 - half * HALF : c1 - half * HALF].rearrange("p j (m u e) -> p m u j e", u=2, e=2)
-            dst = w1_bf[:, :, c0 // PACK : c1 // PACK, :].rearrange("p (u e) m j -> p m u j e", e=2)
-            copy(out=dst, in_=src)
+        def round_w1(copy, half, sets):
+            src = w1_raw[half][:].rearrange("p j (m u e) -> p m u j e", u=2, e=2)
+            dst = w1_bf[:, :, half * HALF // PACK : (half + 1) * HALF // PACK, :]
+            copy(out=dst.rearrange("p (u e) m j -> p m u j e", e=2)[:, :, sets], in_=src[:, :, sets])
 
-        round_w1(nc.scalar.copy, 0, HALF)
-        round_w1(nc.scalar.copy, HALF, HALF + SCALAR_SHARE)
-        round_w1(nc.vector.tensor_copy, HALF + SCALAR_SHARE, H)
+        round_w1(nc.scalar.copy, 0, slice(0, 2))
+        round_w1(nc.vector.tensor_copy, 1, slice(0, 1))
+        round_w1(nc.vector.tensor_copy, 1, slice(1, 2))
         w1c = [sb("w1c%d" % t, [P, P], U32) for t in range(PACK)]
         w1s = [sb("w1s%d" % t, [P, P], U8) for t in range(PACK)]
         h = [sb("h%d" % t, [P, S], F32) for t in range(PACK)]
@@ -96,7 +97,7 @@ def tile_picked_mixup_none_po_kernel(
             nc.vector.quantize_mx(
                 out=w1c[t][:].bitcast(FP8X4), scales=w1s[t][:], in_=w1_bf[:, t].rearrange("p m j -> p (m j)")
             )
-            banks = [0, PACK] if t == 0 else [t]
+            banks = FIRST_BANKS[t]
             width = S // len(banks)
             for i, number in enumerate(banks):
                 cols = slice(i * width, (i + 1) * width)
@@ -117,14 +118,15 @@ def tile_picked_mixup_none_po_kernel(
         )
 
         own = []
-        turned = [bank("turned%d" % c, [P, PACK, P], PACK + c) for c in range(BLOCKS)]
+        turned = [bank("turned%d" % c, [P, PACK, P], TURN_BANKS[c]) for c in range(BLOCKS)]
         for c in range(BLOCKS):
             for t in range(PACK):
                 nc.tensor.transpose(turned[c][:, t, :], h[t][:, c * P : (c + 1) * P], ident[:])
+        stage = sb("stage", [P, BLOCKS, PACK, P], F32)
         for c in range(BLOCKS):
-            scaled = sb("scaled%d" % c, [P, PACK, P], F32)
-            nc.scalar.activation(out=scaled[:], in_=turned[c][:], func=COPY, scale=lam_c[:, c : c + 1])
-            own_c = bank("own%d" % c, [P, PACK, P], c)
+            scaled = stage[:, c]
+            nc.scalar.activation(out=scaled, in_=turned[c][:], func=COPY, scale=lam_c[:, c : c + 1])
+            own_c = bank("own%d" % c, [P, PACK, P], OWN_BANKS[c])
             for t in range(PACK):
                 nc.tensor.transpose(own_c[:, t, :], scaled[:, t, :], ident[:])
             own.append(own_c)
@@ -133,22 +135,23 @@ def tile_picked_mixup_none_po_kernel(
         osc = sb("osc", [P, S], U8)
         out0_v = out_0.rearrange("(p t) j -> p t j", t=PACK)
         out1_v = out_1[0].rearrange("p n t -> p (n t)").bitcast(I32)
-        partner = sb("partner", [P, PACK, S], F32)
-        for t in range(PACK):
-            for j0 in range(0, S, GATHER_W):
-                nc.vector.tensor_tensor(
-                    partner[:, t, j0 : j0 + GATHER_W],
-                    h[t][:].indirect(pos_t[:, j0 // 16 : (j0 + GATHER_W) // 16]),
-                    mu_t[:, j0 : j0 + GATHER_W],
-                    MULT,
-                )
+        early = S - P
+        first = sb("partner", [P, PACK, early], F32)
+        fetched = [first[:, :, c * P : (c + 1) * P] for c in range(BLOCKS - 1)]
+        fetched.append(stage[:, :, 0, :])
+
+        def fetch(out, t, j0, j1):
+            nc.vector.tensor_tensor(out, h[t][:].indirect(pos_t[:, j0 // 16 : j1 // 16]), mu_t[:, j0:j1], MULT)
+
+        def fetch_block(c, t):
+            fetch(fetched[c][:, t, :], t, c * P, (c + 1) * P)
 
         def mix(c):
             z = sb("z%d" % c, [P, P * PACK], BF16)
             nc.vector.tensor_tensor(
                 z[:].rearrange("p (j e t) -> p j t e", e=2, t=PACK),
                 own[c][:].rearrange("p t (j e) -> p j t e", e=2),
-                partner[:, :, c * P : (c + 1) * P].rearrange("p t (j e) -> p j t e", e=2),
+                fetched[c].rearrange("p t (j e) -> p j t e", e=2),
                 ADD,
             )
             return z
@@ -157,11 +160,8 @@ def tile_picked_mixup_none_po_kernel(
             zc = sb("zc%d" % c, [P, P], U32)
             zs = sb("zs%d" % c, [P, P], U8)
             nc.vector.quantize_mx(out=zc[:].bitcast(FP8X4), scales=zs[:], in_=z[:])
-            if c < BLOCKS - 1:
-                y_ps = [bank("y_ps%d" % c, [P, PACK, P], PACK + c)]
-            else:
-                y_ps = [bank("y_ps%d_%d" % (c, t), [P, 1, P], (PACK + c + t) % 8) for t in range(PACK)]
-            rows = PACK // len(y_ps)
+            rows = PACK // len(OUT_BANKS[c])
+            y_ps = [bank("y_ps%d_%d" % (c, number), [P, rows, P], number) for number in OUT_BANKS[c]]
             for t in range(PACK):
                 nc.tensor.matmul_mx(
                     out=y_ps[t // rows][:, t % rows, :],
@@ -171,41 +171,52 @@ def tile_picked_mixup_none_po_kernel(
                 )
             return y_ps
 
+        yb = sb("yb", [P, S, PACK], BF16)
+
         def way_out(c, y_ps):
             j = c * P
             y = sb("y%d" % c, [P, PACK, P], F32)
-            yb = sb("yb%d" % c, [P, P, PACK], BF16)
             rows = PACK // len(y_ps)
             for i, part in enumerate(y_ps):
                 nc.scalar.copy(out=y[:, i * rows : (i + 1) * rows, :], in_=part[:])
             queue = nc.sync if c < BLOCKS - 1 else nc.scalar
             queue.dma_start(out=out0_v[:, :, j : j + P], in_=y[:])
-            nc.vector.tensor_copy(
-                out=yb[:].rearrange("p (j e) t -> p j t e", e=2), in_=y[:].rearrange("p t (j e) -> p j t e", e=2)
-            )
-            return yb
+            if c == 0:
+                nc.scalar.copy(out=yb[:, j : j + P, :], in_=y_ps[0][:].rearrange("p t j -> p j t"))
+            else:
+                nc.vector.tensor_copy(
+                    out=yb[:, j : j + P, :].rearrange("p (j e) t -> p j t e", e=2),
+                    in_=y[:].rearrange("p t (j e) -> p j t e", e=2),
+                )
 
-        def planes(c, yb):
-            j = c * P
+        def planes(j0, j1):
             nc.vector.quantize_mx(
-                out=oc[:, j : j + P].bitcast(FP8X4), scales=osc[:, j : j + P],
-                in_=yb[:].rearrange("p j t -> p (j t)"),
+                out=oc[:, j0:j1].bitcast(FP8X4), scales=osc[:, j0:j1],
+                in_=yb[:, j0:j1, :].rearrange("p j t -> p (j t)"),
             )
-            if c >= BLOCKS - 2:
-                j0 = 0 if c == BLOCKS - 2 else j
-                nc.sync.dma_start(out=out1_v[:, j0 : j + P], in_=oc[:, j0 : j + P])
 
-        z = [mix(0)]
+        for t in range(PACK):
+            fetch(first[:, t, :], t, 0, early)
+        last = BLOCKS - 1
+        fetch_block(last, 0)
         y_ps = []
-        for c in range(BLOCKS):
-            if c + 1 < BLOCKS:
-                z.append(mix(c + 1))
-            y_ps.append(second(c, z[c]))
-        yb = [way_out(0, y_ps[0])]
-        for c in range(BLOCKS):
-            if c + 1 < BLOCKS:
-                yb.append(way_out(c + 1, y_ps[c + 1]))
-            planes(c, yb[c])
+        for c in range(last):
+            z = mix(c)
+            fetch_block(last, c + 1)
+            y_ps.append(second(c, z))
+            if c == 0:
+                way_out(c, y_ps[c])
+        z = mix(last)
+        planes(0, P)
+        y_ps.append(second(last, z))
+        way_out(1, y_ps[1])
+        way_out(2, y_ps[2])
+        planes(P, 2 * P)
+        way_out(last, y_ps[last])
+        planes(2 * P, early)
+        nc.sync.dma_start(out=out1_v[:, 0:early], in_=oc[:, 0:early])
+        planes(early, S)
+        nc.sync.dma_start(out=out1_v[:, early:S], in_=oc[:, early:S])
         for q in range(4):
             queue = nc.sync if q < 2 else nc.scalar
             queue.dma_start(

@@ -19,7 +19,7 @@ MULT = mybir.AluOpType.mult
 ADD = mybir.AluOpType.add
 COPY = mybir.ActivationFunctionType.Copy
 
-HALF = H // 2
+SCALAR_SHARES = (192, 272)
 BLOCKS = S // P
 FIRST_BANKS = ((0, 4), (1,), (2,), (3, 7))
 TURN_BANKS = (5, 6, 3, 7)
@@ -56,7 +56,7 @@ def tile_picked_mixup_none_po_kernel(
         lam_c = sb("lam_c", [P, BLOCKS], F32)
         mu_t = sb("mu_t", [P, S], F32)
         xs = sb("xs", [P, T], U8)
-        w1_raw = [sb("w1_raw%d" % c, [P, PACK, HALF], F32) for c in range(2)]
+        w1_raw = sb("w1_raw", [P, PACK, H], F32)
         ident = sb("ident", [P, P], F32)
         nc.gpsimd.memset(xs[:].bitcast(I32), 0)
         nc.vector.memset(w2s[:].bitcast(I32), 0)
@@ -65,9 +65,7 @@ def tile_picked_mixup_none_po_kernel(
         nc.sync.dma_start(out=xw[:], in_=x_words[0].rearrange("p n t -> p (n t)").bitcast(I32))
         nc.sync.dma_start(offs_t[:], offs)
         load_scales([nc.sync], xs, x_scales)
-        w1_v = w1.rearrange("(p j) c -> p j c", j=PACK)
-        for c in range(2):
-            nc.sync.dma_start(out=w1_raw[c][:], in_=w1_v[:, :, c * HALF : (c + 1) * HALF])
+        nc.sync.dma_start(out=w1_raw[:], in_=w1.rearrange("(p j) c -> p j c", j=PACK))
         nc.sync.dma_start(out=w2w[:], in_=w2_words[0].rearrange("p n t -> p (n t)").bitcast(I32))
         load_scales([nc.sync], w2s, w2_scales)
         nc.sync.dma_start(pos_t[:], pos1)
@@ -82,14 +80,14 @@ def tile_picked_mixup_none_po_kernel(
 
         w1_bf = shared.tile([P, PACK, P, PACK], BF16, name="w1_bf", align_bytes=64, offset=0)
 
-        def round_w1(copy, half, sets):
-            src = w1_raw[half][:].rearrange("p j (m u e) -> p m u j e", u=2, e=2)
-            dst = w1_bf[:, :, half * HALF // PACK : (half + 1) * HALF // PACK, :]
-            copy(out=dst.rearrange("p (u e) m j -> p m u j e", e=2)[:, :, sets], in_=src[:, :, sets])
+        def round_w1(copy, pair, c0, c1):
+            src = w1_raw[:, :, c0:c1].rearrange("p j (m u e) -> p u m j e", u=2, e=2)
+            dst = w1_bf[:, :, c0 // PACK : c1 // PACK, :].rearrange("p (u e) m j -> p u m j e", e=2)
+            copy(out=dst[:, pair], in_=src[:, pair])
 
-        round_w1(nc.scalar.copy, 0, slice(0, 2))
-        round_w1(nc.vector.tensor_copy, 1, slice(0, 1))
-        round_w1(nc.vector.tensor_copy, 1, slice(1, 2))
+        for pair, share in enumerate(SCALAR_SHARES):
+            round_w1(nc.scalar.copy, pair, 0, share)
+            round_w1(nc.vector.tensor_copy, pair, share, H)
         w1c = [sb("w1c%d" % t, [P, P], U32) for t in range(PACK)]
         w1s = [sb("w1s%d" % t, [P, P], U8) for t in range(PACK)]
         h = [sb("h%d" % t, [P, S], F32) for t in range(PACK)]
@@ -212,11 +210,11 @@ def tile_picked_mixup_none_po_kernel(
         way_out(1, y_ps[1])
         way_out(2, y_ps[2])
         planes(P, 2 * P)
+        nc.sync.dma_start(out=out1_v[:, 0 : 2 * P], in_=oc[:, 0 : 2 * P])
         way_out(last, y_ps[last])
         planes(2 * P, early)
-        nc.sync.dma_start(out=out1_v[:, 0:early], in_=oc[:, 0:early])
         planes(early, S)
-        nc.sync.dma_start(out=out1_v[:, early:S], in_=oc[:, early:S])
+        nc.sync.dma_start(out=out1_v[:, 2 * P : S], in_=oc[:, 2 * P : S])
         for q in range(4):
             queue = nc.sync if q < 2 else nc.scalar
             queue.dma_start(

@@ -19,7 +19,7 @@ MULT = mybir.AluOpType.mult
 ADD = mybir.AluOpType.add
 COPY = mybir.ActivationFunctionType.Copy
 
-SCALAR_SHARES = (192, 272)
+SCALAR_SHARES = (240, 272)
 BLOCKS = S // P
 FIRST_BANKS = ((0, 4), (1,), (2,), (3, 7))
 TURN_BANKS = (5, 6, 3, 7)
@@ -109,7 +109,8 @@ def tile_picked_mixup_none_po_kernel(
         w2dw = shared.tile([P, H], I32, name="w2dw", align_bytes=64, offset=0)
         w2ds = shared.tile([P, H], U8, name="w2ds", align_bytes=64, offset=4 * H)
         nc.vector.tensor_copy(
-            out=w2dw[:].rearrange("p (t m) -> p m t", t=PACK), in_=w2w[:].rearrange("p (m t) -> p m t", t=PACK)
+            out=w2dw[:].rearrange("p (t m e) -> p m t e", t=PACK, e=2),
+            in_=w2w[:].rearrange("p (m e t) -> p m t e", t=PACK, e=2),
         )
         nc.vector.tensor_copy(
             out=w2ds[:].rearrange("p (t m) -> p t m", t=PACK), in_=w2s[:].rearrange("p (m t) -> p t m", t=PACK)

@@ -22,9 +22,9 @@ COPY = mybir.ActivationFunctionType.Copy
 SCALAR_SHARES = (240, 272)
 BLOCKS = S // P
 FIRST_BANKS = ((0, 4), (1,), (2,), (3, 7))
-TURN_BANKS = (5, 6, 3, 7)
-OWN_BANKS = (0, 1, 2, 4)
-OUT_BANKS = ((5,), (6,), (3,), (7, 0, 1, 2))
+TURN_BANKS = ((5, 1), (6,), (0,), (4,))
+OWN_BANKS = (2, 3, 7, 5)
+OUT_BANKS = ((1,), (6,), (0,), (4, 2, 3, 7))
 
 
 def tile_picked_mixup_none_po_kernel(
@@ -116,19 +116,35 @@ def tile_picked_mixup_none_po_kernel(
             out=w2ds[:].rearrange("p (t m) -> p t m", t=PACK), in_=w2s[:].rearrange("p (m t) -> p t m", t=PACK)
         )
 
-        own = []
-        turned = [bank("turned%d" % c, [P, PACK, P], TURN_BANKS[c]) for c in range(BLOCKS)]
-        for c in range(BLOCKS):
-            for t in range(PACK):
-                nc.tensor.transpose(turned[c][:, t, :], h[t][:, c * P : (c + 1) * P], ident[:])
+        turned = [
+            [bank("turned%d_%d" % (c, n), [P, PACK // len(TURN_BANKS[c]), P], n) for n in TURN_BANKS[c]]
+            for c in range(BLOCKS)
+        ]
+        own = [bank("own%d" % c, [P, PACK, P], OWN_BANKS[c]) for c in range(BLOCKS)]
         stage = sb("stage", [P, BLOCKS, PACK, P], F32)
-        for c in range(BLOCKS):
-            scaled = stage[:, c]
-            nc.scalar.activation(out=scaled, in_=turned[c][:], func=COPY, scale=lam_c[:, c : c + 1])
-            own_c = bank("own%d" % c, [P, PACK, P], OWN_BANKS[c])
-            for t in range(PACK):
-                nc.tensor.transpose(own_c[:, t, :], scaled[:, t, :], ident[:])
-            own.append(own_c)
+
+        def turn(c, t):
+            rows = PACK // len(turned[c])
+            nc.tensor.transpose(turned[c][t // rows][:, t % rows, :], h[t][:, c * P : (c + 1) * P], ident[:])
+
+        def own_share(c, i):
+            rows = PACK // len(turned[c])
+            scaled = stage[:, c, i * rows : (i + 1) * rows]
+            nc.scalar.activation(out=scaled, in_=turned[c][i][:], func=COPY, scale=lam_c[:, c : c + 1])
+            for t in range(rows):
+                nc.tensor.transpose(own[c][:, i * rows + t, :], scaled[:, t, :], ident[:])
+
+        for t in range(PACK):
+            for c in range(2):
+                turn(c, t)
+        own_share(0, 0)
+        for t in range(PACK):
+            turn(2, t)
+        own_share(0, 1)
+        for t in range(PACK):
+            turn(3, t)
+        own_share(1, 0)
+        own_share(2, 0)
 
         oc = sb("oc", [P, S], I32)
         osc = sb("osc", [P, S], U8)
@@ -204,6 +220,7 @@ def tile_picked_mixup_none_po_kernel(
             fetch_block(last, c + 1)
             y_ps.append(second(c, z))
             if c == 0:
+                own_share(last, 0)
                 way_out(c, y_ps[c])
         z = mix(last)
         planes(0, P)

@@ -24,7 +24,7 @@ BLOCKS = S // P
 FIRST_BANKS = ((0, 4), (1,), (2,), (3, 7))
 TURN_BANKS = ((5, 1), (6,), (0,), (4,))
 OWN_BANKS = (2, 3, 7, 5)
-OUT_BANKS = ((1,), (6,), (0,), (4, 2, 3, 7))
+OUT_BANKS = ((1,), (6,), (0,), (4,), (2, 3))
 
 
 def tile_picked_mixup_none_po_kernel(
@@ -161,22 +161,22 @@ def tile_picked_mixup_none_po_kernel(
         def fetch_block(c, t):
             fetch(fetched[c][:, t, :], t, c * P, (c + 1) * P)
 
-        def mix(c):
-            z = sb("z%d" % c, [P, P * PACK], BF16)
+        def mix(c, j0, j1):
+            z = sb("z%d_%d" % (c, j0), [P, (j1 - j0) * PACK], BF16)
             nc.vector.tensor_tensor(
                 z[:].rearrange("p (j e t) -> p j t e", e=2, t=PACK),
-                own[c][:].rearrange("p t (j e) -> p j t e", e=2),
-                fetched[c].rearrange("p t (j e) -> p j t e", e=2),
+                own[c][:, :, j0:j1].rearrange("p t (j e) -> p j t e", e=2),
+                fetched[c][:, :, j0:j1].rearrange("p t (j e) -> p j t e", e=2),
                 ADD,
             )
             return z
 
-        def second(c, z):
-            zc = sb("zc%d" % c, [P, P], U32)
-            zs = sb("zs%d" % c, [P, P], U8)
+        def second(n, z, width):
+            zc = sb("zc%d" % n, [P, width], U32)
+            zs = sb("zs%d" % n, [P, width], U8)
             nc.vector.quantize_mx(out=zc[:].bitcast(FP8X4), scales=zs[:], in_=z[:])
-            rows = PACK // len(OUT_BANKS[c])
-            y_ps = [bank("y_ps%d_%d" % (c, number), [P, rows, P], number) for number in OUT_BANKS[c]]
+            rows = PACK // len(OUT_BANKS[n])
+            y_ps = [bank("y_ps%d_%d" % (n, number), [P, rows, width], number) for number in OUT_BANKS[n]]
             for t in range(PACK):
                 nc.tensor.matmul_mx(
                     out=y_ps[t // rows][:, t % rows, :],
@@ -187,22 +187,21 @@ def tile_picked_mixup_none_po_kernel(
             return y_ps
 
         yb = sb("yb", [P, S, PACK], BF16)
+        y = [sb("y%d" % c, [P, PACK, P], F32) for c in range(BLOCKS)]
 
-        def way_out(c, y_ps):
-            j = c * P
-            y = sb("y%d" % c, [P, PACK, P], F32)
+        def way_out(c, j0, j1, y_ps):
             rows = PACK // len(y_ps)
             for i, part in enumerate(y_ps):
-                nc.scalar.copy(out=y[:, i * rows : (i + 1) * rows, :], in_=part[:])
-            queue = nc.sync if c < BLOCKS - 1 else nc.scalar
-            queue.dma_start(out=out0_v[:, :, j : j + P], in_=y[:])
-            if c == 0:
-                nc.scalar.copy(out=yb[:, j : j + P, :], in_=y_ps[0][:].rearrange("p t j -> p j t"))
-            else:
-                nc.vector.tensor_copy(
-                    out=yb[:, j : j + P, :].rearrange("p (j e) t -> p j t e", e=2),
-                    in_=y[:].rearrange("p t (j e) -> p j t e", e=2),
-                )
+                nc.scalar.copy(out=y[c][:, i * rows : (i + 1) * rows, j0:j1], in_=part[:])
+            if j1 == P:
+                queue = nc.sync if c < BLOCKS - 1 else nc.scalar
+                queue.dma_start(out=out0_v[:, :, c * P : (c + 1) * P], in_=y[c][:])
+
+        def round_out(c, j0, j1):
+            nc.vector.tensor_copy(
+                out=yb[:, c * P + j0 : c * P + j1, :].rearrange("p (j e) t -> p j t e", e=2),
+                in_=y[c][:, :, j0:j1].rearrange("p t (j e) -> p j t e", e=2),
+            )
 
         def planes(j0, j1):
             nc.vector.quantize_mx(
@@ -213,25 +212,39 @@ def tile_picked_mixup_none_po_kernel(
         for t in range(PACK):
             fetch(first[:, t, :], t, 0, early)
         last = BLOCKS - 1
+        cut = P // 2
         fetch_block(last, 0)
         y_ps = []
         for c in range(last):
-            z = mix(c)
-            fetch_block(last, c + 1)
-            y_ps.append(second(c, z))
+            z = mix(c, 0, P)
+            if c < last - 1:
+                fetch_block(last, c + 1)
+            else:
+                fetch(fetched[last][:, last, 0:cut], last, early, early + cut)
+            y_ps.append(second(c, z, P))
             if c == 0:
                 own_share(last, 0)
-                way_out(c, y_ps[c])
-        z = mix(last)
+                way_out(c, 0, P, y_ps[c])
+                nc.scalar.copy(out=yb[:, 0:P, :], in_=y_ps[c][0][:].rearrange("p t j -> p j t"))
+        z = mix(last, 0, cut)
+        fetch(fetched[last][:, last, cut:P], last, early + cut, S)
+        y_ps.append(second(last, z, cut))
+        z = mix(last, cut, P)
         planes(0, P)
-        y_ps.append(second(last, z))
-        way_out(1, y_ps[1])
-        way_out(2, y_ps[2])
+        y_ps.append(second(last + 1, z, cut))
+        way_out(1, 0, P, y_ps[1])
+        round_out(1, 0, P)
+        way_out(2, 0, P, y_ps[2])
+        round_out(2, 0, P)
         planes(P, 2 * P)
         nc.sync.dma_start(out=out1_v[:, 0 : 2 * P], in_=oc[:, 0 : 2 * P])
-        way_out(last, y_ps[last])
+        way_out(last, 0, cut, y_ps[last])
+        round_out(last, 0, cut)
         planes(2 * P, early)
-        planes(early, S)
+        way_out(last, cut, P, y_ps[last + 1])
+        round_out(last, cut, P)
+        planes(early, early + cut)
+        planes(early + cut, S)
         nc.sync.dma_start(out=out1_v[:, 2 * P : S], in_=oc[:, 2 * P : S])
         for q in range(4):
             queue = nc.sync if q < 2 else nc.scalar

@@ -24,6 +24,7 @@ BLOCKS = S // P
 FIRST_BANKS = ((0, 4), (1,), (2,), (3, 7))
 TURN_BANKS = ((5, 1), (6,), (0,), (4,))
 OWN_BANKS = (2, 3, 7, 5)
+CODE_SLOTS = (1, 2, 7, 0, 3)
 OUT_BANKS = ((1,), (6,), (0,), (4,), (2, 3))
 
 
@@ -34,6 +35,7 @@ def tile_picked_mixup_none_po_kernel(
     with ExitStack() as ctx:
         keep = ctx.enter_context(tc.tile_pool(name="keep", bufs=1))
         shared = ctx.enter_context(tc.tile_pool(name="shared", bufs=1))
+        turns = ctx.enter_context(tc.tile_pool(name="turns", bufs=1))
         psum = ctx.enter_context(tc.psum_pool(name="psum", bufs=1))
 
         def sb(name, shape, dtype, tag=None):
@@ -90,7 +92,9 @@ def tile_picked_mixup_none_po_kernel(
             round_w1(nc.vector.tensor_copy, pair, share, H)
         w1c = [sb("w1c%d" % t, [P, P], U32) for t in range(PACK)]
         w1s = [sb("w1s%d" % t, [P, P], U8) for t in range(PACK)]
-        h = [sb("h%d" % t, [P, S], F32) for t in range(PACK)]
+        h = [
+            turns.tile([P, S], F32, name="h%d" % t, align_bytes=64, offset=(BLOCKS + t) * 4 * S) for t in range(PACK)
+        ]
         for t in range(PACK):
             nc.vector.quantize_mx(
                 out=w1c[t][:].bitcast(FP8X4), scales=w1s[t][:], in_=w1_bf[:, t].rearrange("p m j -> p (m j)")
@@ -121,7 +125,9 @@ def tile_picked_mixup_none_po_kernel(
             for c in range(BLOCKS)
         ]
         own = [bank("own%d" % c, [P, PACK, P], OWN_BANKS[c]) for c in range(BLOCKS)]
-        stage = sb("stage", [P, BLOCKS, PACK, P], F32)
+        stage = [
+            turns.tile([P, PACK, P], F32, name="stage%d" % c, align_bytes=64, offset=c * 4 * S) for c in range(BLOCKS)
+        ]
 
         def turn(c, t):
             rows = PACK // len(turned[c])
@@ -129,7 +135,7 @@ def tile_picked_mixup_none_po_kernel(
 
         def own_share(c, i):
             rows = PACK // len(turned[c])
-            scaled = stage[:, c, i * rows : (i + 1) * rows]
+            scaled = stage[c][:, i * rows : (i + 1) * rows]
             nc.scalar.activation(out=scaled, in_=turned[c][i][:], func=COPY, scale=lam_c[:, c : c + 1])
             for t in range(rows):
                 nc.tensor.transpose(own[c][:, i * rows + t, :], scaled[:, t, :], ident[:])
@@ -145,6 +151,7 @@ def tile_picked_mixup_none_po_kernel(
             turn(3, t)
         own_share(1, 0)
         own_share(2, 0)
+        own_share(3, 0)
 
         oc = sb("oc", [P, S], I32)
         osc = sb("osc", [P, S], U8)
@@ -153,13 +160,12 @@ def tile_picked_mixup_none_po_kernel(
         early = S - P
         first = sb("partner", [P, PACK, early], F32)
         fetched = [first[:, :, c * P : (c + 1) * P] for c in range(BLOCKS - 1)]
-        fetched.append(stage[:, :, 0, :])
+        plain = sb("plain", [P, PACK, P], F32)
+        late = sb("late", [P, PACK, P], F32)
+        fetched.append(late[:])
 
         def fetch(out, t, j0, j1):
             nc.vector.tensor_tensor(out, h[t][:].indirect(pos_t[:, j0 // 16 : j1 // 16]), mu_t[:, j0:j1], MULT)
-
-        def fetch_block(c, t):
-            fetch(fetched[c][:, t, :], t, c * P, (c + 1) * P)
 
         def mix(c, j0, j1):
             z = sb("z%d_%d" % (c, j0), [P, (j1 - j0) * PACK], BF16)
@@ -172,7 +178,7 @@ def tile_picked_mixup_none_po_kernel(
             return z
 
         def second(n, z, width):
-            zc = sb("zc%d" % n, [P, width], U32)
+            zc = turns.tile([P, width], U32, name="zc%d" % n, align_bytes=64, offset=CODE_SLOTS[n] * 4 * S)
             zs = sb("zs%d" % n, [P, width], U8)
             nc.vector.quantize_mx(out=zc[:].bitcast(FP8X4), scales=zs[:], in_=z[:])
             rows = PACK // len(OUT_BANKS[n])
@@ -213,27 +219,26 @@ def tile_picked_mixup_none_po_kernel(
             fetch(first[:, t, :], t, 0, early)
         last = BLOCKS - 1
         cut = P // 2
-        fetch_block(last, 0)
-        y_ps = []
-        for c in range(last):
-            z = mix(c, 0, P)
-            if c < last - 1:
-                fetch_block(last, c + 1)
-            else:
-                fetch(fetched[last][:, last, 0:cut], last, early, early + cut)
-            y_ps.append(second(c, z, P))
-            if c == 0:
-                own_share(last, 0)
-                way_out(c, 0, P, y_ps[c])
-                nc.scalar.copy(out=yb[:, 0:P, :], in_=y_ps[c][0][:].rearrange("p t j -> p j t"))
-        z = mix(last, 0, cut)
-        fetch(fetched[last][:, last, cut:P], last, early + cut, S)
-        y_ps.append(second(last, z, cut))
-        z = mix(last, cut, P)
-        planes(0, P)
-        y_ps.append(second(last + 1, z, cut))
+        for t in range(PACK):
+            nc.scalar.activation(out=plain[:, t, :], in_=h[t][:].indirect(pos_t[:, early // 16 : S // 16]), func=COPY)
+        z0 = mix(0, 0, P)
+        z1 = mix(1, 0, P)
+        y_ps = [second(0, z0, P)]
+        way_out(0, 0, P, y_ps[0])
+        z2 = mix(2, 0, P)
+        y_ps.append(second(1, z1, P))
         way_out(1, 0, P, y_ps[1])
+        nc.vector.tensor_tensor(
+            late[:], plain[:], mu_t[:, early:S].unsqueeze(1).to_broadcast([P, PACK, P]), MULT
+        )
+        y_ps.append(second(2, z2, P))
+        z3a = mix(last, 0, cut)
+        z3b = mix(last, cut, P)
+        y_ps.append(second(last, z3a, cut))
+        y_ps.append(second(last + 1, z3b, cut))
+        round_out(0, 0, P)
         round_out(1, 0, P)
+        planes(0, P)
         way_out(2, 0, P, y_ps[2])
         round_out(2, 0, P)
         planes(P, 2 * P)

@@ -24,7 +24,7 @@ BLOCKS = S // P
 FIRST_BANKS = ((0, 4), (1,), (2,), (3, 7))
 TURN_BANKS = ((5, 1), (6,), (0,), (4,))
 OWN_BANKS = (2, 3, 7, 5)
-CODE_SLOTS = (1, 2, 7, 0, 3)
+CODE_SLOTS = (0, 1, 2, 12, 13)
 OUT_BANKS = ((1,), (6,), (0,), (4,), (2, 3))
 
 
@@ -125,9 +125,17 @@ def tile_picked_mixup_none_po_kernel(
             for c in range(BLOCKS)
         ]
         own = [bank("own%d" % c, [P, PACK, P], OWN_BANKS[c]) for c in range(BLOCKS)]
-        stage = [
-            turns.tile([P, PACK, P], F32, name="stage%d" % c, align_bytes=64, offset=c * 4 * S) for c in range(BLOCKS)
-        ]
+        early = S - P
+        pitch = 7 * P
+        wide = sb("wide", [P, 2 * S + PACK * pitch], F32)
+        first = wide[:, 0 : PACK * early].rearrange("p (t j) -> p t j", t=PACK)
+        stage = {
+            (c, 0): turns.tile([P, PACK, P], F32, name="stage%d" % c, align_bytes=64, offset=c * 4 * S)[:]
+            for c in range(2, BLOCKS)
+        }
+        stage[1, 0] = wide[:, 2 * S :].rearrange("p (t j) -> p t j", t=PACK)[:, :, 0:P]
+        stage[0, 0] = wide[:, PACK * early + P : PACK * early + early].rearrange("p (t j) -> p t j", t=2)
+        stage[0, 1] = wide[:, PACK * early - P : PACK * early + P].rearrange("p (t j) -> p t j", t=2)
 
         def turn(c, t):
             rows = PACK // len(turned[c])
@@ -135,9 +143,9 @@ def tile_picked_mixup_none_po_kernel(
 
         def own_share(c, i):
             rows = PACK // len(turned[c])
-            scaled = stage[c][:, i * rows : (i + 1) * rows]
+            scaled = stage[c, i]
             nc.scalar.activation(out=scaled, in_=turned[c][i][:], func=COPY, scale=lam_c[:, c : c + 1])
-            for t in range(rows):
+            for t in reversed(range(rows)):
                 nc.tensor.transpose(own[c][:, i * rows + t, :], scaled[:, t, :], ident[:])
 
         for t in range(PACK):
@@ -157,8 +165,6 @@ def tile_picked_mixup_none_po_kernel(
         osc = sb("osc", [P, S], U8)
         out0_v = out_0.rearrange("(p t) j -> p t j", t=PACK)
         out1_v = out_1[0].rearrange("p n t -> p (n t)").bitcast(I32)
-        early = S - P
-        first = sb("partner", [P, PACK, early], F32)
         fetched = [first[:, :, c * P : (c + 1) * P] for c in range(BLOCKS - 1)]
         plain = sb("plain", [P, PACK, P], F32)
         late = sb("late", [P, PACK, P], F32)
@@ -178,7 +184,7 @@ def tile_picked_mixup_none_po_kernel(
             return z
 
         def second(n, z, width):
-            zc = turns.tile([P, width], U32, name="zc%d" % n, align_bytes=64, offset=CODE_SLOTS[n] * 4 * S)
+            zc = turns.tile([P, width], U32, name="zc%d" % n, align_bytes=64, offset=CODE_SLOTS[n] * 4 * P)
             zs = sb("zs%d" % n, [P, width], U8)
             nc.vector.quantize_mx(out=zc[:].bitcast(FP8X4), scales=zs[:], in_=z[:])
             rows = PACK // len(OUT_BANKS[n])
@@ -216,29 +222,38 @@ def tile_picked_mixup_none_po_kernel(
             )
 
         for t in range(PACK):
-            fetch(first[:, t, :], t, 0, early)
+            width = early if t < 2 else 2 * P
+            fetch(first[:, t, 0:width], t, 0, width)
         last = BLOCKS - 1
         cut = P // 2
         for t in range(PACK):
             nc.scalar.activation(out=plain[:, t, :], in_=h[t][:].indirect(pos_t[:, early // 16 : S // 16]), func=COPY)
         z0 = mix(0, 0, P)
-        z1 = mix(1, 0, P)
+        fetch(first[:, 3, 2 * P : early], 3, 2 * P, early)
         y_ps = [second(0, z0, P)]
         way_out(0, 0, P, y_ps[0])
-        z2 = mix(2, 0, P)
+        nc.scalar.copy(out=yb[:, 0:P, :], in_=y_ps[0][0][:].rearrange("p t j -> p j t"))
+        z1 = mix(1, 0, P)
+        fetch(first[:, 2, 2 * P : early], 2, 2 * P, early)
         y_ps.append(second(1, z1, P))
         way_out(1, 0, P, y_ps[1])
-        nc.vector.tensor_tensor(
-            late[:], plain[:], mu_t[:, early:S].unsqueeze(1).to_broadcast([P, PACK, P]), MULT
-        )
+        z2 = mix(2, 0, P)
+
+        def weigh(j0, j1):
+            nc.vector.tensor_tensor(
+                late[:, :, j0:j1], plain[:, :, j0:j1],
+                mu_t[:, early + j0 : early + j1].unsqueeze(1).to_broadcast([P, PACK, j1 - j0]), MULT,
+            )
+
+        weigh(0, cut)
         y_ps.append(second(2, z2, P))
         z3a = mix(last, 0, cut)
-        z3b = mix(last, cut, P)
+        weigh(cut, P)
         y_ps.append(second(last, z3a, cut))
-        y_ps.append(second(last + 1, z3b, cut))
-        round_out(0, 0, P)
-        round_out(1, 0, P)
+        z3b = mix(last, cut, P)
         planes(0, P)
+        y_ps.append(second(last + 1, z3b, cut))
+        round_out(1, 0, P)
         way_out(2, 0, P, y_ps[2])
         round_out(2, 0, P)
         planes(P, 2 * P)

@@ -139,7 +139,15 @@ def tile_picked_mixup_none_po_kernel(
 
         def turn(c, t):
             rows = PACK // len(turned[c])
-            nc.tensor.transpose(turned[c][t // rows][:, t % rows, :], h[t][:, c * P : (c + 1) * P], ident[:])
+            out = turned[c][t // rows][:, t % rows, :]
+            cols = slice(c * P, (c + 1) * P)
+            if t == PACK - 1 and c < BLOCKS - 1:
+                nc.tensor.matmul_mx(
+                    out=out, lhsT=xqw[:, cols].bitcast(FP8X4), lhsT_scale=xqs[:, cols],
+                    rhs=w1c[t][:].bitcast(FP8X4), rhs_scale=w1s[t][:], start=True, stop=True,
+                )
+            else:
+                nc.tensor.transpose(out, h[t][:, cols], ident[:])
 
         def own_share(c, i):
             rows = PACK // len(turned[c])

@@ -24,7 +24,7 @@ BLOCKS = S // P
 FIRST_BANKS = ((0, 4), (1,), (2,), (3, 7))
 TURN_BANKS = ((5, 1), (6,), (0,), (4,))
 OWN_BANKS = (2, 3, 7, 5)
-CODE_SLOTS = (0, 1, 2, 12, 13)
+CODE_SLOTS = (0, 8, 2, 12, 13)
 OUT_BANKS = ((1,), (6,), (0,), (4,), (2, 3))
 
 
@@ -126,14 +126,13 @@ def tile_picked_mixup_none_po_kernel(
         ]
         own = [bank("own%d" % c, [P, PACK, P], OWN_BANKS[c]) for c in range(BLOCKS)]
         early = S - P
-        pitch = 7 * P
-        wide = sb("wide", [P, 2 * S + PACK * pitch], F32)
+        wide = sb("wide", [P, (PACK + 1) * early], F32)
         first = wide[:, 0 : PACK * early].rearrange("p (t j) -> p t j", t=PACK)
         stage = {
             (c, 0): turns.tile([P, PACK, P], F32, name="stage%d" % c, align_bytes=64, offset=c * 4 * S)[:]
             for c in range(2, BLOCKS)
         }
-        stage[1, 0] = wide[:, 2 * S :].rearrange("p (t j) -> p t j", t=PACK)[:, :, 0:P]
+        stage[1, 0] = sb("stage1", [P, PACK, P], F32)[:]
         stage[0, 0] = wide[:, PACK * early + P : PACK * early + early].rearrange("p (t j) -> p t j", t=2)
         stage[0, 1] = wide[:, PACK * early - P : PACK * early + P].rearrange("p (t j) -> p t j", t=2)
 
@@ -232,6 +231,7 @@ def tile_picked_mixup_none_po_kernel(
         for t in range(PACK):
             width = early if t < 2 else 2 * P
             fetch(first[:, t, 0:width], t, 0, width)
+        fetch(first[:, 2, 2 * P : early], 2, 2 * P, early)
         last = BLOCKS - 1
         cut = P // 2
         for t in range(PACK):
@@ -242,10 +242,9 @@ def tile_picked_mixup_none_po_kernel(
         way_out(0, 0, P, y_ps[0])
         nc.scalar.copy(out=yb[:, 0:P, :], in_=y_ps[0][0][:].rearrange("p t j -> p j t"))
         z1 = mix(1, 0, P)
-        fetch(first[:, 2, 2 * P : early], 2, 2 * P, early)
+        z2 = mix(2, 0, P)
         y_ps.append(second(1, z1, P))
         way_out(1, 0, P, y_ps[1])
-        z2 = mix(2, 0, P)
 
         def weigh(j0, j1):
             nc.vector.tensor_tensor(

@@ -180,10 +180,11 @@ def tile_picked_mixup_none_po_kernel(
         def fetch(out, t, j0, j1):
             nc.vector.tensor_tensor(out, h[t][:].indirect(pos_t[:, j0 // 16 : j1 // 16]), mu_t[:, j0:j1], MULT)
 
-        def mix(c, j0, j1):
-            z = sb("z%d_%d" % (c, j0), [P, (j1 - j0) * PACK], BF16)
+        def mix(c, j0, j1, z=None):
+            if z is None:
+                z = sb("z%d_%d" % (c, j0), [P, (j1 - j0) * PACK], BF16)[:]
             nc.vector.tensor_tensor(
-                z[:].rearrange("p (j e t) -> p j t e", e=2, t=PACK),
+                z.rearrange("p (j e t) -> p j t e", e=2, t=PACK),
                 own[c][:, :, j0:j1].rearrange("p t (j e) -> p j t e", e=2),
                 fetched[c][:, :, j0:j1].rearrange("p t (j e) -> p j t e", e=2),
                 ADD,
@@ -193,7 +194,7 @@ def tile_picked_mixup_none_po_kernel(
         def second(n, z, width):
             zc = turns.tile([P, width], U32, name="zc%d" % n, align_bytes=64, offset=CODE_SLOTS[n] * 4 * P)
             zs = sb("zs%d" % n, [P, width], U8)
-            nc.vector.quantize_mx(out=zc[:].bitcast(FP8X4), scales=zs[:], in_=z[:])
+            nc.vector.quantize_mx(out=zc[:].bitcast(FP8X4), scales=zs[:], in_=z)
             rows = PACK // len(OUT_BANKS[n])
             y_ps = [bank("y_ps%d_%d" % (n, number), [P, rows, width], number) for number in OUT_BANKS[n]]
             for t in range(PACK):
@@ -240,11 +241,12 @@ def tile_picked_mixup_none_po_kernel(
         fetch(first[:, 3, 2 * P : early], 3, 2 * P, early)
         y_ps = [second(0, z0, P)]
         way_out(0, 0, P, y_ps[0])
-        nc.scalar.copy(out=yb[:, 0:P, :], in_=y_ps[0][0][:].rearrange("p t j -> p j t"))
         z1 = mix(1, 0, P)
-        z2 = mix(2, 0, P)
+        z2 = sb("z2", [P, P * PACK], BF16)[:]
+        mix(2, 0, cut, z2[:, 0 : cut * PACK])
         y_ps.append(second(1, z1, P))
         way_out(1, 0, P, y_ps[1])
+        mix(2, cut, P, z2[:, cut * PACK :])
 
         def weigh(j0, j1):
             nc.vector.tensor_tensor(
@@ -258,9 +260,10 @@ def tile_picked_mixup_none_po_kernel(
         weigh(cut, P)
         y_ps.append(second(last, z3a, cut))
         z3b = mix(last, cut, P)
-        planes(0, P)
+        round_out(0, 0, P)
         y_ps.append(second(last + 1, z3b, cut))
         round_out(1, 0, P)
+        planes(0, P)
         way_out(2, 0, P, y_ps[2])
         round_out(2, 0, P)
         planes(P, 2 * P)

from contextlib import ExitStack

import concourse.mybir as mybir
from concourse.masks import make_identity

K, T, S, H = 512, 1024, 512, 512
P = 128
PACK = 4
FLOPS = 2 * K * H * S + 2 * H * H * S

F32 = mybir.dt.float32
BF16 = mybir.dt.bfloat16
I32 = mybir.dt.int32
U32 = mybir.dt.uint32
U16 = mybir.dt.uint16
U8 = mybir.dt.uint8
FP8X4 = mybir.dt.float8_e4m3fn_x4
MULT = mybir.AluOpType.mult
ADD = mybir.AluOpType.add
COPY = mybir.ActivationFunctionType.Copy

SCALAR_SHARES = (240, 272)
BLOCKS = S // P
FIRST_BANKS = ((0, 4), (1,), (2,), (3, 7))
TURN_BANKS = ((5, 1), (6,), (0,), (4,))
OWN_BANKS = (2, 3, 7, 5)
CODE_SLOTS = (0, 8, 2, 12, 13)
OUT_BANKS = ((1,), (6,), (0,), (4,), (2, 3))


def tile_picked_mixup_none_po_kernel(
    tc, x_words, x_scales, w1, w2_words, w2_scales, lam, mu, offs, pos1, out_0, out_1, out_2
):
    nc = tc.nc
    with ExitStack() as ctx:
        keep = ctx.enter_context(tc.tile_pool(name="keep", bufs=1))
        shared = ctx.enter_context(tc.tile_pool(name="shared", bufs=1))
        turns = ctx.enter_context(tc.tile_pool(name="turns", bufs=1))
        psum = ctx.enter_context(tc.psum_pool(name="psum", bufs=1))

        def sb(name, shape, dtype, tag=None):
            return keep.tile(shape, dtype, name=name, tag=tag or name, align_bytes=64)

        def bank(name, shape, number):
            return psum.tile(shape, F32, name=name, tag="bank%d" % number)

        def load_scales(queues, tile, scales):
            for q in range(4):
                queues[q % len(queues)].dma_start(
                    out=tile[32 * q : 32 * q + 4, :].bitcast(I32), in_=scales[0, 4 * q : 4 * q + 4, :].bitcast(I32)
                )

        offs_t = sb("offs_t", [P, S // 16], U16)
        pos_t = sb("pos_t", [P, S // 16], U16)
        xw = sb("xw", [P, T], I32)
        w2w = sb("w2w", [P, H], I32)
        w2s = sb("w2s", [P, H], U8)
        lam_c = sb("lam_c", [P, BLOCKS], F32)
        mu_t = sb("mu_t", [P, S], F32)
        xs = sb("xs", [P, T], U8)
        w1_raw = sb("w1_raw", [P, PACK, H], F32)
        ident = sb("ident", [P, P], F32)
        nc.gpsimd.memset(xs[:].bitcast(I32), 0)
        nc.vector.memset(w2s[:].bitcast(I32), 0)
        make_identity(nc, ident[:])

        nc.sync.dma_start(out=xw[:], in_=x_words[0].rearrange("p n t -> p (n t)").bitcast(I32))
        nc.sync.dma_start(offs_t[:], offs)
        load_scales([nc.sync], xs, x_scales)
        nc.sync.dma_start(out=w1_raw[:], in_=w1.rearrange("(p j) c -> p j c", j=PACK))
        nc.sync.dma_start(out=w2w[:], in_=w2_words[0].rearrange("p n t -> p (n t)").bitcast(I32))
        load_scales([nc.sync], w2s, w2_scales)
        nc.sync.dma_start(pos_t[:], pos1)
        nc.sync.dma_start(out=mu_t[:], in_=mu)
        with nc.allow_non_contiguous_dma(reason="one value of lam for each partition and block"):
            nc.sync.dma_start(out=lam_c[:], in_=lam[0, :].rearrange("(c p) -> p c", p=P))

        xqw = sb("xqw", [P, S], U32)
        xqs = sb("xqs", [P, S], U8)
        nc.vector.tensor_copy(xqw[:], xw[:].bitcast(U32).indirect(offs_t[:]))
        nc.vector.tensor_copy(xqs[:], xs[:].indirect(offs_t[:]))

        w1_bf = shared.tile([P, PACK, P, PACK], BF16, name="w1_bf", align_bytes=64, offset=0)

        def round_w1(copy, pair, c0, c1):
            src = w1_raw[:, :, c0:c1].rearrange("p j (m u e) -> p u m j e", u=2, e=2)
            dst = w1_bf[:, :, c0 // PACK : c1 // PACK, :].rearrange("p (u e) m j -> p u m j e", e=2)
            copy(out=dst[:, pair], in_=src[:, pair])

        for pair, share in enumerate(SCALAR_SHARES):
            round_w1(nc.scalar.copy, pair, 0, share)
            round_w1(nc.vector.tensor_copy, pair, share, H)
        w1c = [sb("w1c%d" % t, [P, P], U32) for t in range(PACK)]
        w1s = [sb("w1s%d" % t, [P, P], U8) for t in range(PACK)]
        h = [
            turns.tile([P, S], F32, name="h%d" % t, align_bytes=64, offset=(BLOCKS + t) * 4 * S) for t in range(PACK)
        ]
        for t in range(PACK):
            nc.vector.quantize_mx(
                out=w1c[t][:].bitcast(FP8X4), scales=w1s[t][:], in_=w1_bf[:, t].rearrange("p m j -> p (m j)")
            )
            banks = FIRST_BANKS[t]
            width = S // len(banks)
            for i, number in enumerate(banks):
                cols = slice(i * width, (i + 1) * width)
                h_ps = bank("h_ps%d_%d" % (t, i), [P, width], number)
                nc.tensor.matmul_mx(
                    out=h_ps[:], lhsT=w1c[t][:].bitcast(FP8X4), lhsT_scale=w1s[t][:],
                    rhs=xqw[:, cols].bitcast(FP8X4), rhs_scale=xqs[:, cols], start=True, stop=True,
                )
                nc.scalar.copy(out=h[t][:, cols], in_=h_ps[:])

        w2dw = shared.tile([P, H], I32, name="w2dw", align_bytes=64, offset=0)
        w2ds = shared.tile([P, H], U8, name="w2ds", align_bytes=64, offset=4 * H)
        nc.vector.tensor_copy(
            out=w2dw[:].rearrange("p (t m e) -> p m t e", t=PACK, e=2),
            in_=w2w[:].rearrange("p (m e t) -> p m t e", t=PACK, e=2),
        )
        nc.vector.tensor_copy(
            out=w2ds[:].rearrange("p (t m) -> p t m", t=PACK), in_=w2s[:].rearrange("p (m t) -> p t m", t=PACK)
        )

        turned = [
            [bank("turned%d_%d" % (c, n), [P, PACK // len(TURN_BANKS[c]), P], n) for n in TURN_BANKS[c]]
            for c in range(BLOCKS)
        ]
        own = [bank("own%d" % c, [P, PACK, P], OWN_BANKS[c]) for c in range(BLOCKS)]
        early = S - P
        wide = sb("wide", [P, (PACK + 1) * early], F32)
        first = wide[:, 0 : PACK * early].rearrange("p (t j) -> p t j", t=PACK)
        stage = {
            (c, 0): turns.tile([P, PACK, P], F32, name="stage%d" % c, align_bytes=64, offset=c * 4 * S)[:]
            for c in range(2, BLOCKS)
        }
        stage[1, 0] = sb("stage1", [P, PACK, P], F32)[:]
        stage[0, 0] = wide[:, PACK * early + P : PACK * early + early].rearrange("p (t j) -> p t j", t=2)
        stage[0, 1] = wide[:, PACK * early - P : PACK * early + P].rearrange("p (t j) -> p t j", t=2)

        def turn(c, t):
            rows = PACK // len(turned[c])
            out = turned[c][t // rows][:, t % rows, :]
            cols = slice(c * P, (c + 1) * P)
            if t == PACK - 1 and c < BLOCKS - 1:
                nc.tensor.matmul_mx(
                    out=out, lhsT=xqw[:, cols].bitcast(FP8X4), lhsT_scale=xqs[:, cols],
                    rhs=w1c[t][:].bitcast(FP8X4), rhs_scale=w1s[t][:], start=True, stop=True,
                )
            else:
                nc.tensor.transpose(out, h[t][:, cols], ident[:])

        def own_share(c, i):
            rows = PACK // len(turned[c])
            scaled = stage[c, i]
            nc.scalar.activation(out=scaled, in_=turned[c][i][:], func=COPY, scale=lam_c[:, c : c + 1])
            for t in reversed(range(rows)):
                nc.tensor.transpose(own[c][:, i * rows + t, :], scaled[:, t, :], ident[:])

        for t in range(PACK):
            for c in range(2):
                turn(c, t)
        own_share(0, 0)
        for t in range(PACK):
            turn(2, t)
        own_share(0, 1)
        for t in range(PACK):
            turn(3, t)
        own_share(1, 0)
        own_share(2, 0)
        own_share(3, 0)

        oc = sb("oc", [P, S], I32)
        osc = sb("osc", [P, S], U8)
        out0_v = out_0.rearrange("(p t) j -> p t j", t=PACK)
        out1_v = out_1[0].rearrange("p n t -> p (n t)").bitcast(I32)
        fetched = [first[:, :, c * P : (c + 1) * P] for c in range(BLOCKS - 1)]
        plain = sb("plain", [P, PACK, P], F32)
        late = sb("late", [P, PACK, P], F32)
        fetched.append(late[:])

        def fetch(out, t, j0, j1):
            nc.vector.tensor_tensor(out, h[t][:].indirect(pos_t[:, j0 // 16 : j1 // 16]), mu_t[:, j0:j1], MULT)

        def mix(c, j0, j1, z=None):
            if z is None:
                z = sb("z%d_%d" % (c, j0), [P, (j1 - j0) * PACK], BF16)[:]
            nc.vector.tensor_tensor(
                z.rearrange("p (j e t) -> p j t e", e=2, t=PACK),
                own[c][:, :, j0:j1].rearrange("p t (j e) -> p j t e", e=2),
                fetched[c][:, :, j0:j1].rearrange("p t (j e) -> p j t e", e=2),
                ADD,
            )
            return z

        def second(n, z, width):
            zc = turns.tile([P, width], U32, name="zc%d" % n, align_bytes=64, offset=CODE_SLOTS[n] * 4 * P)
            zs = sb("zs%d" % n, [P, width], U8)
            nc.vector.quantize_mx(out=zc[:].bitcast(FP8X4), scales=zs[:], in_=z)
            rows = PACK // len(OUT_BANKS[n])
            y_ps = [bank("y_ps%d_%d" % (n, number), [P, rows, width], number) for number in OUT_BANKS[n]]
            for t in range(PACK):
                nc.tensor.matmul_mx(
                    out=y_ps[t // rows][:, t % rows, :],
                    lhsT=w2dw[:, t * P : (t + 1) * P].bitcast(FP8X4), lhsT_scale=w2ds[:, t * P : (t + 1) * P],
                    rhs=zc[:].bitcast(FP8X4), rhs_scale=zs[:],
                    start=True, stop=True,
                )
            return y_ps

        yb = sb("yb", [P, S, PACK], BF16)
        y = [sb("y%d" % c, [P, PACK, P], F32) for c in range(BLOCKS)]

        def way_out(c, j0, j1, y_ps):
            rows = PACK // len(y_ps)
            for i, part in enumerate(y_ps):
                nc.scalar.copy(out=y[c][:, i * rows : (i + 1) * rows, j0:j1], in_=part[:])
            if j1 == P:
                queue = nc.sync if c < BLOCKS - 1 else nc.scalar
                queue.dma_start(out=out0_v[:, :, c * P : (c + 1) * P], in_=y[c][:])

        def round_out(c, j0, j1):
            nc.vector.tensor_copy(
                out=yb[:, c * P + j0 : c * P + j1, :].rearrange("p (j e) t -> p j t e", e=2),
                in_=y[c][:, :, j0:j1].rearrange("p t (j e) -> p j t e", e=2),
            )

        def planes(j0, j1):
            nc.vector.quantize_mx(
                out=oc[:, j0:j1].bitcast(FP8X4), scales=osc[:, j0:j1],
                in_=yb[:, j0:j1, :].rearrange("p j t -> p (j t)"),
            )

        for t in range(PACK):
            width = early if t < 2 else 2 * P
            fetch(first[:, t, 0:width], t, 0, width)
        fetch(first[:, 2, 2 * P : early], 2, 2 * P, early)
        last = BLOCKS - 1
        cut = P // 2
        for t in range(PACK):
            nc.scalar.activation(out=plain[:, t, :], in_=h[t][:].indirect(pos_t[:, early // 16 : S // 16]), func=COPY)
        z0 = mix(0, 0, P)
        fetch(first[:, 3, 2 * P : early], 3, 2 * P, early)
        y_ps = [second(0, z0, P)]
        way_out(0, 0, P, y_ps[0])
        z1 = mix(1, 0, P)
        z2 = sb("z2", [P, P * PACK], BF16)[:]
        mix(2, 0, cut, z2[:, 0 : cut * PACK])
        y_ps.append(second(1, z1, P))
        way_out(1, 0, P, y_ps[1])
        mix(2, cut, P, z2[:, cut * PACK :])

        def weigh(j0, j1):
            nc.vector.tensor_tensor(
                late[:, :, j0:j1], plain[:, :, j0:j1],
                mu_t[:, early + j0 : early + j1].unsqueeze(1).to_broadcast([P, PACK, j1 - j0]), MULT,
            )

        weigh(0, cut)
        y_ps.append(second(2, z2, P))
        z3a = mix(last, 0, cut)
        weigh(cut, P)
        y_ps.append(second(last, z3a, cut))
        z3b = mix(last, cut, P)
        round_out(0, 0, P)
        y_ps.append(second(last + 1, z3b, cut))
        round_out(1, 0, P)
        planes(0, P)
        way_out(2, 0, P, y_ps[2])
        round_out(2, 0, P)
        planes(P, 2 * P)
        nc.sync.dma_start(out=out1_v[:, 0 : 2 * P], in_=oc[:, 0 : 2 * P])
        way_out(last, 0, cut, y_ps[last])
        round_out(last, 0, cut)
        planes(2 * P, early)
        way_out(last, cut, P, y_ps[last + 1])
        round_out(last, cut, P)
        planes(early, early + cut)
        planes(early + cut, S)
        nc.sync.dma_start(out=out1_v[:, 2 * P : S], in_=oc[:, 2 * P : S])
        for q in range(4):
            queue = nc.sync if q < 2 else nc.scalar
            queue.dma_start(
                out=out_2[0, 4 * q : 4 * q + 4, :].bitcast(I32), in_=osc[32 * q : 32 * q + 4, :].bitcast(I32)
            )
